import numpy as np
import ml_dtypes


def mxq(x, axis, fmt="e4m3"):
    dtype, down = {"e4m3": (ml_dtypes.float8_e4m3fn, 7), "e5m2": (ml_dtypes.float8_e5m2, 14)}[fmt]
    v = np.moveaxis(np.asarray(x, np.float32).astype(ml_dtypes.bfloat16).astype(np.float64), axis, -1)
    blocks = v.reshape(v.shape[:-1] + (-1, 32))
    amax = np.abs(blocks).max(-1, keepdims=True)
    byte = np.maximum(np.where(amax > 0, np.frexp(amax)[1] - 1 + 127, 0) - down, 1)
    scale = np.exp2(byte - 127.0)
    codes = (blocks / scale).astype(np.float32).astype(dtype).astype(np.float64)
    return np.moveaxis((codes * scale).reshape(v.shape), -1, axis)


WIDE = False


def mx_kscale(k):
    if not WIDE:
        return np.ones(k)
    levels = np.array([24, -24, 12, -12, 0])
    if k % 512:
        return np.exp2(np.random.permutation(np.resize(levels, k // 32))).repeat(32)
    a = np.empty((k // 512, 16))
    for p in range(k // 512):
        a[p, :8] = np.random.permutation(np.resize(levels, 8))
        for g in range(8):
            far = levels[np.abs(levels - a[p, g]) >= 10]
            a[p, g + 8] = far[np.random.randint(len(far))]
    return np.exp2(a.ravel()).repeat(32)


def f64(x):
    return np.asarray(x).astype(np.float64)


def striped(idx):
    return np.tile(idx.reshape(-1, 16).T, (8, 1)).astype(np.uint16)


def unstriped(offs):
    return offs[:16].T.reshape(-1).astype(np.int64)


E2M1 = np.array([0.0, 0.5, 1.0, 1.5, 2.0, 3.0, 4.0, 6.0, -0.0, -0.5, -1.0, -1.5, -2.0, -3.0, -4.0, -6.0])


def pack_weight(w, fmt):
    k, n = w.shape
    w = f64(np.asarray(w, np.float32).astype(ml_dtypes.bfloat16)).reshape(k // 32, 32, n)
    amax = np.abs(w).max(1)
    if fmt == "e4m3":
        byte = np.frexp(amax)[1] - 1 + 127 - 7
    else:
        mant, ex = np.frexp(amax / 6.0)
        byte = np.where(mant > 0.5, ex, ex - 1) + 127
    byte = np.clip(np.where(amax > 0, byte, 1), 1, 254)
    scaled = (w * np.exp2(127.0 - byte)[:, None, :]).reshape(k, n).astype(np.float32)
    by_word = np.ascontiguousarray(scaled.reshape(k // 512, 128, 4, n).transpose(0, 1, 3, 2))
    if fmt == "e4m3":
        words = by_word.astype(ml_dtypes.float8_e4m3fn).view(np.uint8)
    else:
        c = by_word.astype(ml_dtypes.float4_e2m1fn).view(np.uint8) & 0xF
        words = (c[..., 0::2] | (c[..., 1::2] << 4)).reshape(k // 512, 128, 2 * n)
    return np.ascontiguousarray(words), np.ascontiguousarray(byte.astype(np.uint8).reshape(k // 512, 16, n))


def unpack_weight(words, scales, fmt):
    g, _, n = scales.shape
    words = np.ascontiguousarray(words).reshape(g, 128, n, -1)
    if fmt == "e4m3":
        vals = words.view(ml_dtypes.float8_e4m3fn).astype(np.float64)
    else:
        nib = np.empty((g, 128, n, 4), np.uint8)
        nib[..., 0::2] = words & 0xF
        nib[..., 1::2] = words >> 4
        vals = E2M1[nib]
    vals = vals * np.repeat(np.exp2(scales.astype(np.float64) - 127.0), 8, axis=1)[..., None]
    return vals.transpose(0, 1, 3, 2).reshape(g * 512, n)


def pack_table4(v):
    words, scales = pack_weight(v, "e2m1")
    g, t = words.shape[0] // 2, v.shape[1]
    return np.ascontiguousarray(words.reshape(g, 2, 128, t, 2).transpose(0, 2, 3, 1, 4).reshape(g, 128, t, 4)), scales


def unpack_table4(words, scales):
    g, _, t, _ = words.shape
    return unpack_weight(words.reshape(g, 128, t, 2, 2).transpose(0, 3, 1, 2, 4).reshape(2 * g, 128, 2 * t), scales, "e2m1")


K, R, M, N, T, J = 1024, 512, 256, 512, 4096, 1024


def setup_inputs():
    n = np.random.standard_normal
    s = mx_kscale(K)[:, None]
    s2 = mx_kscale(K)[:, None]
    u = mx_kscale(R)[:, None]
    p_tab = pack_table4(n((K, T)) * s2)
    p_wk = pack_weight(n((K, R)) / np.sqrt(K) / s2 * u.T, "e4m3")
    return {
        "tab_words": p_tab[0],
        "tab_scales": p_tab[1],
        "x": (n((K, M)) * s).astype(np.float32),
        "wq": (n((K, R)) / np.sqrt(K) / s / u.T).astype(np.float32),
        "wk_words": p_wk[0],
        "wk_scales": p_wk[1],
        "wv": (n((K, N)) / np.sqrt(K) / s2).astype(np.float32),
        "offs": striped(np.random.permutation(T)[:J]),
    }


def reference(tab_words, tab_scales, x, wq, wk_words, wk_scales, wv, offs):
    idx = unstriped(offs)
    tab_ = unpack_table4(tab_words, tab_scales)[:, idx]
    x_ = mxq(f64(x), 0, "e4m3")
    wq_ = mxq(f64(wq), 0, "e4m3")
    wk_ = unpack_weight(wk_words, wk_scales, "e4m3")
    qr = wq_.T @ x_
    kr = wk_.T @ tab_
    qa = np.maximum(qr, 0.0)
    ka = np.maximum(kr, 0.0)
    qa_ = mxq(qa, 0, "e4m3")
    ka_ = mxq(ka, 0, "e4m3")
    sc = qa_.T @ ka_
    wv_ = mxq(f64(wv), 0, "e4m3")
    vv = wv_.T @ tab_
    return sc * 0.03125, vv

@@ -1,0 +1,227 @@
+from contextlib import ExitStack
+
+import concourse.mybir as mybir
+
+K, R, M, N, T, J = 1024, 512, 256, 512, 4096, 1024
+FLOPS = 2 * K * R * M + 2 * K * R * J + 2 * R * M * J + 2 * K * N * J
+
+F32 = mybir.dt.float32
+BF16 = mybir.dt.bfloat16
+I32 = mybir.dt.int32
+U32 = mybir.dt.uint32
+U16 = mybir.dt.uint16
+U8 = mybir.dt.uint8
+FP8X4 = mybir.dt.float8_e4m3fn_x4
+FP4X4 = mybir.dt.float4_e2m1fn_x4
+RELU = mybir.ActivationFunctionType.Relu
+COPY = mybir.ActivationFunctionType.Copy
+MULT = mybir.AluOpType.mult
+
+P = 128
+PACK = 4
+K_PASS = P * PACK
+PASSES = K // K_PASS
+BANK = 512
+HALVES = J // BANK
+SHIFT = 16
+SCORE_SCALE = 0.03125
+
+
+def tile_list_kvt_act_kernel(
+    tc, tab_words, tab_scales, x, wq, wk_words, wk_scales, wv, offs, out_0, out_1
+):
+    nc = tc.nc
+    with ExitStack() as ctx:
+        keep = ctx.enter_context(tc.tile_pool(name="keep", bufs=1))
+        stage = ctx.enter_context(tc.tile_pool(name="stage", bufs=3))
+        psum = ctx.enter_context(tc.psum_pool(name="psum", bufs=8))
+
+        def held(shape, dtype, name):
+            return keep.tile(shape, dtype, name=name, align_bytes=64)
+
+        offsets = keep.tile([P, J // 16], U16, name="offsets")
+        nc.sync.dma_start(offsets[:], offs)
+
+        scale_win = held([P, T // 4], I32, "scale_win")
+        nc.vector.memset(scale_win[:], 0)
+        scale_rows = tab_scales.rearrange("a (q r) t -> r q a t", r=4)
+        for r in range(4):
+            nc.scalar.dma_start(scale_win[r:P:SHIFT, :], scale_rows[r].bitcast(I32))
+
+        wk_raw = held([P, PASSES, R], I32, "wk_raw")
+        nc.sync.dma_start(wk_raw[:], wk_words.rearrange("a p r i -> p a (r i)").bitcast(I32))
+
+        wk_scale_raw = held([P, PASSES, R // 4], I32, "wk_scale_raw")
+        nc.gpsimd.memset(wk_scale_raw[:], 0)
+        for q in range(4):
+            nc.gpsimd.dma_start(
+                wk_scale_raw[32 * q : 32 * q + 4, :, :],
+                wk_scales[:, 4 * q : 4 * q + 4, :].rearrange("a r c -> r a c").bitcast(I32),
+            )
+
+        word_win = held([P, T], I32, "word_win")
+        nc.sync.dma_start(word_win[:], tab_words[0].rearrange("p t b -> p (t b)").bitcast(I32))
+
+        def load_pass(src, a, name):
+            width = src.shape[1]
+            raw = stage.tile([P, PACK, width], F32, name=name, tag="raw")
+            rows = src[a * K_PASS : (a + 1) * K_PASS, :]
+            nc.sync.dma_start(raw[:], rows.rearrange("(p s) w -> p s w", s=PACK))
+            return raw
+
+        wv_raw = [load_pass(wv, a, "wv_raw%d" % a) for a in range(PASSES)]
+        wq_raw0 = load_pass(wq, 0, "wq_raw0")
+
+        wk_codes = held([P, PASSES, R], I32, "wk_codes")
+        nc.vector.tensor_copy(
+            wk_codes[:].rearrange("p a (t g i) -> p a t g i", t=4, i=4),
+            wk_raw[:].rearrange("p a (g t i) -> p a t g i", t=4, i=4),
+        )
+        moved_plane = held([P, J // 4], I32, "moved_plane")
+        nc.vector.memset(moved_plane[:], 0)
+
+        picked_plane = held([P, J], U8, "picked_plane")
+        nc.vector.tensor_copy(picked_plane[:], scale_win[:].bitcast(U8).indirect(offsets[:]))
+        nc.gpsimd.dma_start(moved_plane[0 : P - SHIFT, :], picked_plane[SHIFT:P, :].bitcast(I32))
+        tab_planes = [picked_plane[:], moved_plane[:].bitcast(U8)]
+
+        wk_plane = held([P, PASSES, R // 4], I32, "wk_plane")
+        nc.vector.tensor_copy(
+            wk_plane[:].rearrange("p a (t g) -> p a t g", t=4),
+            wk_scale_raw[:].rearrange("p a (g t) -> p a t g", t=4),
+        )
+
+        def quantize(grouped, name):
+            width = grouped.shape[1] // PACK
+            codes = held([P, width], U32, name + "_codes")
+            plane = held([P, width], U8, name + "_plane")
+            nc.vector.quantize_mx(out=codes[:].bitcast(FP8X4), scales=plane[:], in_=grouped[:])
+            return codes, plane
+
+        def interleave(raw, name, engine_copy):
+            grouped = held([P, PACK * raw.shape[2]], BF16, name)
+            engine_copy(
+                grouped[:].rearrange("p (c i s) -> p c s i", i=4, s=PACK),
+                raw[:].rearrange("p s (c i) -> p c s i", i=4),
+            )
+            return grouped
+
+        def interleave_wq(raw, name, engine_copy):
+            grouped = held([P, PACK * R], BF16, name)
+            engine_copy(
+                grouped[:].rearrange("p (t g i s) -> p t g s i", t=4, i=4, s=PACK),
+                raw[:].rearrange("p s (g t i) -> p t g s i", t=4, i=4),
+            )
+            return grouped
+
+        tab_codes = []
+        ka_grouped = []
+        for h in range(HALVES):
+            picked = held([P, BANK], U32, "picked%d" % h)
+            cols = slice(h * BANK // 16, (h + 1) * BANK // 16)
+            nc.vector.tensor_copy(picked[:], word_win[:].bitcast(U32).indirect(offsets[:, cols]))
+            codes = held([P, PASSES, 2 * BANK], U8, "tab_codes%d" % h)
+            nc.vector.tensor_copy(
+                codes[:].bitcast(U16),
+                picked[:].bitcast(U16).rearrange("p (j d) -> p d j", d=PASSES),
+            )
+            tab_codes.append(codes)
+
+            grouped = held([P, PACK * BANK], BF16, "ka_grouped%d" % h)
+            for b in range(BANK // P):
+                bank = psum.tile([P, PACK, P], F32, name="k_bank", tag="bank")
+                for t in range(PACK):
+                    for a in range(PASSES):
+                        nc.tensor.matmul_mx(
+                            out=bank[:, t, :],
+                            lhsT=wk_codes[:, a, t * P : (t + 1) * P].bitcast(FP8X4),
+                            lhsT_scale=wk_plane[:, a, :].bitcast(U8)[:, t * P : (t + 1) * P],
+                            rhs=codes[:, a, 2 * b * P : 2 * (b + 1) * P].bitcast(FP4X4),
+                            rhs_scale=tab_planes[a][:, h * BANK + b * P : h * BANK + (b + 1) * P],
+                            start=(a == 0),
+                            stop=(a == PASSES - 1),
+                        )
+                nc.scalar.activation(
+                    grouped[:, b * BANK : (b + 1) * BANK].rearrange("p (j t) -> p j t", t=PACK),
+                    bank[:].rearrange("p t j -> p j t"),
+                    RELU,
+                )
+            ka_grouped.append(grouped)
+
+        wv_grouped0 = interleave(wv_raw[0], "wv_grouped0", nc.vector.tensor_copy)
+        wq_raw1 = load_pass(wq, 1, "wq_raw1")
+        wv_grouped1 = interleave(wv_raw[1], "wv_grouped1", nc.vector.tensor_copy)
+        x_raw = stage.tile([P, PASSES, PACK, M], F32, name="x_raw", tag="raw")
+        for a in range(PASSES):
+            rows = x[a * K_PASS : (a + 1) * K_PASS, :]
+            nc.sync.dma_start(x_raw[:, a, :, :], rows.rearrange("(p s) w -> p s w", s=PACK))
+        wv_mx = [quantize(wv_grouped0, "wv0"), quantize(wv_grouped1, "wv1")]
+
+        for nb in range(N // P):
+            staged = held([P, J], F32, "vv_staged%d" % nb)
+            for h in range(HALVES):
+                bank = psum.tile([P, BANK], F32, name="v_bank", tag="bank")
+                for a in range(PASSES):
+                    nc.tensor.matmul_mx(
+                        out=bank[:],
+                        lhsT=wv_mx[a][0][:, nb * P : (nb + 1) * P].bitcast(FP8X4),
+                        lhsT_scale=wv_mx[a][1][:, nb * P : (nb + 1) * P],
+                        rhs=tab_codes[h][:, a, :].bitcast(FP4X4),
+                        rhs_scale=tab_planes[a][:, h * BANK : (h + 1) * BANK],
+                        start=(a == 0),
+                        stop=(a == PASSES - 1),
+                    )
+                nc.scalar.copy(staged[:, h * BANK : (h + 1) * BANK], bank[:])
+            nc.sync.dma_start(out_1[nb * P : (nb + 1) * P, :], staged[:])
+
+        wq_grouped0 = interleave_wq(wq_raw0, "wq_grouped0", nc.vector.tensor_copy)
+        ka_mx = [quantize(ka_grouped[0], "ka0")]
+        wq_mx = [quantize(wq_grouped0, "wq0")]
+        ka_mx.append(quantize(ka_grouped[1], "ka1"))
+        wq_grouped1 = interleave_wq(wq_raw1, "wq_grouped1", nc.vector.tensor_copy)
+        x_grouped0 = interleave(x_raw[:, 0, :, :], "x_grouped0", nc.vector.tensor_copy)
+        wq_mx.append(quantize(wq_grouped1, "wq1"))
+        x_grouped1 = interleave(x_raw[:, 1, :, :], "x_grouped1", nc.vector.tensor_copy)
+        x_mx = [quantize(x_grouped0, "x0"), quantize(x_grouped1, "x1")]
+
+        qa_mx = []
+        for mb in range(M // P):
+            bank = psum.tile([P, PACK, P], F32, name="q_bank", tag="bank")
+            for t in range(PACK):
+                for a in range(PASSES):
+                    nc.tensor.matmul_mx(
+                        out=bank[:, t, :],
+                        lhsT=wq_mx[a][0][:, t * P : (t + 1) * P].bitcast(FP8X4),
+                        lhsT_scale=wq_mx[a][1][:, t * P : (t + 1) * P],
+                        rhs=x_mx[a][0][:, mb * P : (mb + 1) * P].bitcast(FP8X4),
+                        rhs_scale=x_mx[a][1][:, mb * P : (mb + 1) * P],
+                        start=(a == 0),
+                        stop=(a == PASSES - 1),
+                    )
+            grouped = held([P, PACK * P], BF16, "qa_grouped%d" % mb)
+            nc.scalar.activation(
+                grouped[:].rearrange("p (m t) -> p m t", t=PACK),
+                bank[:].rearrange("p t m -> p m t"),
+                RELU,
+            )
+            qa_mx.append(quantize(grouped, "qa%d" % mb))
+
+        for mb in range(M // P):
+            staged = held([P, J], F32, "sc_staged%d" % mb)
+            for h in range(HALVES):
+                bank = psum.tile([P, BANK], F32, name="s_bank", tag="bank")
+                nc.tensor.matmul_mx(
+                    out=bank[:],
+                    lhsT=qa_mx[mb][0][:].bitcast(FP8X4),
+                    lhsT_scale=qa_mx[mb][1][:],
+                    rhs=ka_mx[h][0][:].bitcast(FP8X4),
+                    rhs_scale=ka_mx[h][1][:],
+                    start=True,
+                    stop=True,
+                )
+                cols = slice(h * BANK, (h + 1) * BANK)
+                if h == 0:
+                    nc.scalar.activation(staged[:, cols], bank[:], COPY, scale=SCORE_SCALE)
+                else:
+                    nc.vector.tensor_scalar(staged[:, cols], bank[:], SCORE_SCALE, None, MULT)
+            nc.sync.dma_start(out_0[mb * P : (mb + 1) * P, :], staged[:])

@@ -15,6 +15,7 @@ FP8X4 = mybir.dt.float8_e4m3fn_x4
 FP4X4 = mybir.dt.float4_e2m1fn_x4
 RELU = mybir.ActivationFunctionType.Relu
 COPY = mybir.ActivationFunctionType.Copy
+MAX = mybir.AluOpType.max
 MULT = mybir.AluOpType.mult
 
 P = 128
@@ -33,7 +34,7 @@ def tile_list_kvt_act_kernel(
     nc = tc.nc
     with ExitStack() as ctx:
         keep = ctx.enter_context(tc.tile_pool(name="keep", bufs=1))
-        stage = ctx.enter_context(tc.tile_pool(name="stage", bufs=3))
+        shared = ctx.enter_context(tc.tile_pool(name="shared", bufs=1))
         psum = ctx.enter_context(tc.psum_pool(name="psum", bufs=8))
 
         def held(shape, dtype, name):
@@ -42,51 +43,59 @@ def tile_list_kvt_act_kernel(
         offsets = keep.tile([P, J // 16], U16, name="offsets")
         nc.sync.dma_start(offsets[:], offs)
 
-        scale_win = held([P, T // 4], I32, "scale_win")
-        nc.vector.memset(scale_win[:], 0)
-        scale_rows = tab_scales.rearrange("a (q r) t -> r q a t", r=4)
-        for r in range(4):
-            nc.scalar.dma_start(scale_win[r:P:SHIFT, :], scale_rows[r].bitcast(I32))
-
         wk_raw = held([P, PASSES, R], I32, "wk_raw")
         nc.sync.dma_start(wk_raw[:], wk_words.rearrange("a p r i -> p a (r i)").bitcast(I32))
 
-        wk_scale_raw = held([P, PASSES, R // 4], I32, "wk_scale_raw")
-        nc.gpsimd.memset(wk_scale_raw[:], 0)
-        for q in range(4):
-            nc.gpsimd.dma_start(
-                wk_scale_raw[32 * q : 32 * q + 4, :, :],
-                wk_scales[:, 4 * q : 4 * q + 4, :].rearrange("a r c -> r a c").bitcast(I32),
-            )
+        scale_win = shared.tile([P, T // 4], I32, name="scale_win", tag="shared", align_bytes=64)
+        scale_rows = tab_scales.rearrange("a q t -> (a q) t").bitcast(I32)
+        nc.sync.dma_start(scale_win[0:32, :], scale_rows)
+        for q, queue in ((1, nc.sync), (2, nc.sync), (3, nc.scalar)):
+            queue.dma_start(scale_win[28 * q + 4 : 28 * q + 32, :], scale_rows[4:32, :])
+        nc.scalar.dma_start(scale_win[116:P, :], scale_rows[0:12, :])
 
         word_win = held([P, T], I32, "word_win")
         nc.sync.dma_start(word_win[:], tab_words[0].rearrange("p t b -> p (t b)").bitcast(I32))
 
-        def load_pass(src, a, name):
-            width = src.shape[1]
-            raw = stage.tile([P, PACK, width], F32, name=name, tag="raw")
+        wk_scale_raw = held([P, PASSES, R // 4], I32, "wk_scale_raw")
+        nc.gpsimd.memset(wk_scale_raw[:], 0)
+        for q in range(4):
+            nc.sync.dma_start(
+                wk_scale_raw[32 * q : 32 * q + 4, :, :],
+                wk_scales[:, 4 * q : 4 * q + 4, :].rearrange("a r c -> r a c").bitcast(I32),
+            )
+
+        def load_pass(raw, src, a):
             rows = src[a * K_PASS : (a + 1) * K_PASS, :]
-            nc.sync.dma_start(raw[:], rows.rearrange("(p s) w -> p s w", s=PACK))
+            nc.sync.dma_start(raw, rows.rearrange("(p s) w -> p s w", s=PACK))
             return raw
 
-        wv_raw = [load_pass(wv, a, "wv_raw%d" % a) for a in range(PASSES)]
-        wq_raw0 = load_pass(wq, 0, "wq_raw0")
+        x_raw = [load_pass(held([P, PACK, M], F32, "x_first")[:], x, 0)]
 
         wk_codes = held([P, PASSES, R], I32, "wk_codes")
         nc.vector.tensor_copy(
             wk_codes[:].rearrange("p a (t g i) -> p a t g i", t=4, i=4),
             wk_raw[:].rearrange("p a (g t i) -> p a t g i", t=4, i=4),
         )
+
         moved_plane = held([P, J // 4], I32, "moved_plane")
-        nc.vector.memset(moved_plane[:], 0)
+        nc.gpsimd.memset(moved_plane[:], 0)
 
         picked_plane = held([P, J], U8, "picked_plane")
         nc.vector.tensor_copy(picked_plane[:], scale_win[:].bitcast(U8).indirect(offsets[:]))
-        nc.gpsimd.dma_start(moved_plane[0 : P - SHIFT, :], picked_plane[SHIFT:P, :].bitcast(I32))
+        nc.sync.dma_start(moved_plane[0 : P - SHIFT, :], picked_plane[SHIFT:P, :].bitcast(I32))
         tab_planes = [picked_plane[:], moved_plane[:].bitcast(U8)]
 
+        later = shared.tile([P, PACK * (M + PASSES * (R + N))], F32, name="later", tag="shared", align_bytes=64)
+
+        def part(start, width):
+            return later[:, PACK * start : PACK * (start + width)].rearrange("p (s w) -> p s w", s=PACK)
+
+        x_raw.append(load_pass(part(0, M), x, 1))
+        wv_raw = [load_pass(part(M + a * N, N), wv, a) for a in range(PASSES)]
+        wq_raw = [load_pass(part(M + PASSES * N + a * R, R), wq, a) for a in range(PASSES)]
+
         wk_plane = held([P, PASSES, R // 4], I32, "wk_plane")
-        nc.vector.tensor_copy(
+        nc.gpsimd.tensor_copy(
             wk_plane[:].rearrange("p a (t g) -> p a t g", t=4),
             wk_scale_raw[:].rearrange("p a (g t) -> p a t g", t=4),
         )
@@ -102,7 +111,7 @@ def tile_list_kvt_act_kernel(
             grouped = held([P, PACK * raw.shape[2]], BF16, name)
             engine_copy(
                 grouped[:].rearrange("p (c i s) -> p c s i", i=4, s=PACK),
-                raw[:].rearrange("p s (c i) -> p c s i", i=4),
+                raw.rearrange("p s (c i) -> p c s i", i=4),
             )
             return grouped
 
@@ -110,23 +119,25 @@ def tile_list_kvt_act_kernel(
             grouped = held([P, PACK * R], BF16, name)
             engine_copy(
                 grouped[:].rearrange("p (t g i s) -> p t g s i", t=4, i=4, s=PACK),
-                raw[:].rearrange("p s (g t i) -> p t g s i", t=4, i=4),
+                raw.rearrange("p s (g t i) -> p t g s i", t=4, i=4),
             )
             return grouped
 
-        tab_codes = []
-        ka_grouped = []
-        for h in range(HALVES):
+        def gather_words(h):
             picked = held([P, BANK], U32, "picked%d" % h)
             cols = slice(h * BANK // 16, (h + 1) * BANK // 16)
             nc.vector.tensor_copy(picked[:], word_win[:].bitcast(U32).indirect(offsets[:, cols]))
+            return picked
+
+        def part_words(picked, h):
             codes = held([P, PASSES, 2 * BANK], U8, "tab_codes%d" % h)
             nc.vector.tensor_copy(
                 codes[:].bitcast(U16),
                 picked[:].bitcast(U16).rearrange("p (j d) -> p d j", d=PASSES),
             )
-            tab_codes.append(codes)
+            return codes
 
+        def keys(codes, h):
             grouped = held([P, PACK * BANK], BF16, "ka_grouped%d" % h)
             for b in range(BANK // P):
                 bank = psum.tile([P, PACK, P], F32, name="k_bank", tag="bank")
@@ -146,18 +157,9 @@ def tile_list_kvt_act_kernel(
                     bank[:].rearrange("p t j -> p j t"),
                     RELU,
                 )
-            ka_grouped.append(grouped)
+            return grouped
 
-        wv_grouped0 = interleave(wv_raw[0], "wv_grouped0", nc.vector.tensor_copy)
-        wq_raw1 = load_pass(wq, 1, "wq_raw1")
-        wv_grouped1 = interleave(wv_raw[1], "wv_grouped1", nc.vector.tensor_copy)
-        x_raw = stage.tile([P, PASSES, PACK, M], F32, name="x_raw", tag="raw")
-        for a in range(PASSES):
-            rows = x[a * K_PASS : (a + 1) * K_PASS, :]
-            nc.sync.dma_start(x_raw[:, a, :, :], rows.rearrange("(p s) w -> p s w", s=PACK))
-        wv_mx = [quantize(wv_grouped0, "wv0"), quantize(wv_grouped1, "wv1")]
-
-        for nb in range(N // P):
+        def values(nb):
             staged = held([P, J], F32, "vv_staged%d" % nb)
             for h in range(HALVES):
                 bank = psum.tile([P, BANK], F32, name="v_bank", tag="bank")
@@ -174,18 +176,7 @@ def tile_list_kvt_act_kernel(
                 nc.scalar.copy(staged[:, h * BANK : (h + 1) * BANK], bank[:])
             nc.sync.dma_start(out_1[nb * P : (nb + 1) * P, :], staged[:])
 
-        wq_grouped0 = interleave_wq(wq_raw0, "wq_grouped0", nc.vector.tensor_copy)
-        ka_mx = [quantize(ka_grouped[0], "ka0")]
-        wq_mx = [quantize(wq_grouped0, "wq0")]
-        ka_mx.append(quantize(ka_grouped[1], "ka1"))
-        wq_grouped1 = interleave_wq(wq_raw1, "wq_grouped1", nc.vector.tensor_copy)
-        x_grouped0 = interleave(x_raw[:, 0, :, :], "x_grouped0", nc.vector.tensor_copy)
-        wq_mx.append(quantize(wq_grouped1, "wq1"))
-        x_grouped1 = interleave(x_raw[:, 1, :, :], "x_grouped1", nc.vector.tensor_copy)
-        x_mx = [quantize(x_grouped0, "x0"), quantize(x_grouped1, "x1")]
-
-        qa_mx = []
-        for mb in range(M // P):
+        def queries(mb):
             bank = psum.tile([P, PACK, P], F32, name="q_bank", tag="bank")
             for t in range(PACK):
                 for a in range(PASSES):
@@ -199,29 +190,51 @@ def tile_list_kvt_act_kernel(
                         stop=(a == PASSES - 1),
                     )
             grouped = held([P, PACK * P], BF16, "qa_grouped%d" % mb)
-            nc.scalar.activation(
-                grouped[:].rearrange("p (m t) -> p m t", t=PACK),
-                bank[:].rearrange("p t m -> p m t"),
-                RELU,
-            )
-            qa_mx.append(quantize(grouped, "qa%d" % mb))
+            out = grouped[:].rearrange("p (m t) -> p m t", t=PACK)
+            sums = bank[:].rearrange("p t m -> p m t")
+            if mb == 0:
+                nc.vector.tensor_scalar(out, sums, 0.0, None, MAX)
+            else:
+                nc.scalar.activation(out, sums, RELU)
+            return grouped
 
-        for mb in range(M // P):
+        def scores(qa, mb):
             staged = held([P, J], F32, "sc_staged%d" % mb)
             for h in range(HALVES):
                 bank = psum.tile([P, BANK], F32, name="s_bank", tag="bank")
                 nc.tensor.matmul_mx(
                     out=bank[:],
-                    lhsT=qa_mx[mb][0][:].bitcast(FP8X4),
-                    lhsT_scale=qa_mx[mb][1][:],
+                    lhsT=qa[0][:].bitcast(FP8X4),
+                    lhsT_scale=qa[1][:],
                     rhs=ka_mx[h][0][:].bitcast(FP8X4),
                     rhs_scale=ka_mx[h][1][:],
                     start=True,
                     stop=True,
                 )
-                cols = slice(h * BANK, (h + 1) * BANK)
                 if h == 0:
-                    nc.scalar.activation(staged[:, cols], bank[:], COPY, scale=SCORE_SCALE)
+                    nc.scalar.activation(staged[:, 0:BANK], bank[:], COPY, scale=SCORE_SCALE)
                 else:
-                    nc.vector.tensor_scalar(staged[:, cols], bank[:], SCORE_SCALE, None, MULT)
-            nc.sync.dma_start(out_0[mb * P : (mb + 1) * P, :], staged[:])
+                    nc.vector.tensor_scalar(staged[:, BANK:J], bank[:], SCORE_SCALE, None, MULT)
+                cols = slice(h * BANK, (h + 1) * BANK)
+                nc.sync.dma_start(out_0[mb * P : (mb + 1) * P, cols], staged[:, cols])
+
+        on_vector, on_scalar = nc.vector.tensor_copy, nc.scalar.copy
+        tab_codes = [part_words(gather_words(0), 0)]
+        x_grouped = [interleave(x_raw[a], "x_grouped%d" % a, on_scalar) for a in range(PASSES)]
+        ka_grouped = [keys(tab_codes[0], 0)]
+        tab_codes.append(part_words(gather_words(1), 1))
+        ka_grouped.append(keys(tab_codes[1], 1))
+        x_mx = [quantize(x_grouped[a], "x%d" % a) for a in range(PASSES)]
+        wv_grouped = [interleave(wv_raw[a], "wv_grouped%d" % a, on_vector) for a in range(PASSES)]
+        wv_mx = [quantize(wv_grouped[a], "wv%d" % a) for a in range(PASSES)]
+        ka_mx = [quantize(ka_grouped[0], "ka0")]
+        for nb in range(N // P):
+            values(nb)
+        wq_grouped0 = interleave_wq(wq_raw[0], "wq_grouped0", on_vector)
+        ka_mx.append(quantize(ka_grouped[1], "ka1"))
+        wq_mx = [quantize(wq_grouped0, "wq0")]
+        wq_mx.append(quantize(interleave_wq(wq_raw[1], "wq_grouped1", on_vector), "wq1"))
+        qa_grouped = [queries(mb) for mb in range(M // P)]
+        qa_mx = [quantize(qa_grouped[mb], "qa%d" % mb) for mb in range(M // P)]
+        for mb in range(M // P):
+            scores(qa_mx[mb], mb)

@@ -25,6 +25,7 @@ PASSES = K // K_PASS
 BANK = 512
 HALVES = J // BANK
 SHIFT = 16
+HALF = 256
 SCORE_SCALE = 0.03125
 
 
@@ -43,83 +44,80 @@ def tile_list_kvt_act_kernel(
         offsets = keep.tile([P, J // 16], U16, name="offsets")
         nc.sync.dma_start(offsets[:], offs)
 
+        scale_win = held([P, T // 4], I32, "scale_win")
+        nc.vector.memset(scale_win[:], 0)
+        wk_scale_raw = held([P, PASSES, R // 4], I32, "wk_scale_raw")
+        nc.vector.memset(wk_scale_raw[:], 0)
+        moved_plane = held([P, J // 4], I32, "moved_plane")
+        nc.vector.memset(moved_plane[:], 0)
+
         wk_raw = held([P, PASSES, R], I32, "wk_raw")
         nc.sync.dma_start(wk_raw[:], wk_words.rearrange("a p r i -> p a (r i)").bitcast(I32))
 
-        scale_win = shared.tile([P, T // 4], I32, name="scale_win", tag="shared", align_bytes=64)
-        scale_rows = tab_scales.rearrange("a q t -> (a q) t").bitcast(I32)
-        nc.sync.dma_start(scale_win[0:32, :], scale_rows)
-        for q, queue in ((1, nc.sync), (2, nc.sync), (3, nc.scalar)):
-            queue.dma_start(scale_win[28 * q + 4 : 28 * q + 32, :], scale_rows[4:32, :])
-        nc.scalar.dma_start(scale_win[116:P, :], scale_rows[0:12, :])
+        scale_rows = tab_scales.rearrange("a (q e) t -> e q a t", e=4).bitcast(I32)
+        for e in range(4):
+            nc.sync.dma_start(scale_win[e:P:SHIFT, :], scale_rows[e])
 
         word_win = held([P, T], I32, "word_win")
         nc.sync.dma_start(word_win[:], tab_words[0].rearrange("p t b -> p (t b)").bitcast(I32))
 
-        wk_scale_raw = held([P, PASSES, R // 4], I32, "wk_scale_raw")
-        nc.gpsimd.memset(wk_scale_raw[:], 0)
         for q in range(4):
             nc.sync.dma_start(
                 wk_scale_raw[32 * q : 32 * q + 4, :, :],
                 wk_scales[:, 4 * q : 4 * q + 4, :].rearrange("a r c -> r a c").bitcast(I32),
             )
 
-        def load_pass(raw, src, a):
+        def load_pass(src, a, name):
+            raw = held([P, PACK, src.shape[1]], F32, name)
             rows = src[a * K_PASS : (a + 1) * K_PASS, :]
-            nc.sync.dma_start(raw, rows.rearrange("(p s) w -> p s w", s=PACK))
+            nc.sync.dma_start(raw[:], rows.rearrange("(p s) w -> p s w", s=PACK))
             return raw
 
-        x_raw = [load_pass(held([P, PACK, M], F32, "x_first")[:], x, 0)]
+        x_raw = [load_pass(x, a, "x_raw%d" % a) for a in range(PASSES)]
+        wv_raw = [load_pass(wv, a, "wv_raw%d" % a) for a in range(PASSES)]
+        wq_raw = [load_pass(wq, a, "wq_raw%d" % a) for a in range(PASSES)]
+
+        picked_plane = held([P, J], U8, "picked_plane")
+        nc.vector.tensor_copy(picked_plane[:], scale_win[:].bitcast(U8).indirect(offsets[:]))
+        nc.scalar.dma_start(moved_plane[0 : P - SHIFT, :], picked_plane[SHIFT:P, :].bitcast(I32))
+        tab_planes = [picked_plane[:], moved_plane[:].bitcast(U8)]
 
         wk_codes = held([P, PASSES, R], I32, "wk_codes")
         nc.vector.tensor_copy(
             wk_codes[:].rearrange("p a (t g i) -> p a t g i", t=4, i=4),
             wk_raw[:].rearrange("p a (g t i) -> p a t g i", t=4, i=4),
         )
-
-        moved_plane = held([P, J // 4], I32, "moved_plane")
-        nc.gpsimd.memset(moved_plane[:], 0)
-
-        picked_plane = held([P, J], U8, "picked_plane")
-        nc.vector.tensor_copy(picked_plane[:], scale_win[:].bitcast(U8).indirect(offsets[:]))
-        nc.sync.dma_start(moved_plane[0 : P - SHIFT, :], picked_plane[SHIFT:P, :].bitcast(I32))
-        tab_planes = [picked_plane[:], moved_plane[:].bitcast(U8)]
-
-        later = shared.tile([P, PACK * (M + PASSES * (R + N))], F32, name="later", tag="shared", align_bytes=64)
-
-        def part(start, width):
-            return later[:, PACK * start : PACK * (start + width)].rearrange("p (s w) -> p s w", s=PACK)
-
-        x_raw.append(load_pass(part(0, M), x, 1))
-        wv_raw = [load_pass(part(M + a * N, N), wv, a) for a in range(PASSES)]
-        wq_raw = [load_pass(part(M + PASSES * N + a * R, R), wq, a) for a in range(PASSES)]
-
         wk_plane = held([P, PASSES, R // 4], I32, "wk_plane")
-        nc.gpsimd.tensor_copy(
-            wk_plane[:].rearrange("p a (t g) -> p a t g", t=4),
-            wk_scale_raw[:].rearrange("p a (g t) -> p a t g", t=4),
-        )
 
-        def quantize(grouped, name):
+        def deal_wk_scales():
+            nc.vector.tensor_copy(
+                wk_plane[:].rearrange("p a (t g) -> p a t g", t=4),
+                wk_scale_raw[:].rearrange("p a (g t) -> p a t g", t=4),
+            )
+
+        def quantize(grouped, name, tag=None):
             width = grouped.shape[1] // PACK
-            codes = held([P, width], U32, name + "_codes")
+            if tag is None:
+                codes = held([P, width], U32, name + "_codes")
+            else:
+                codes = shared.tile([P, width], U32, name=name + "_codes", tag=tag, align_bytes=64)
             plane = held([P, width], U8, name + "_plane")
             nc.vector.quantize_mx(out=codes[:].bitcast(FP8X4), scales=plane[:], in_=grouped[:])
             return codes, plane
 
         def interleave(raw, name, engine_copy):
-            grouped = held([P, PACK * raw.shape[2]], BF16, name)
+            grouped = shared.tile([P, PACK * raw.shape[2]], BF16, name=name, tag=name, align_bytes=64)
             engine_copy(
                 grouped[:].rearrange("p (c i s) -> p c s i", i=4, s=PACK),
                 raw.rearrange("p s (c i) -> p c s i", i=4),
             )
             return grouped
 
-        def interleave_wq(raw, name, engine_copy):
-            grouped = held([P, PACK * R], BF16, name)
+        def interleave_wq(raw, u, name, engine_copy):
+            grouped = held([P, PACK * HALF], BF16, name)
             engine_copy(
-                grouped[:].rearrange("p (t g i s) -> p t g s i", t=4, i=4, s=PACK),
-                raw.rearrange("p s (g t i) -> p t g s i", t=4, i=4),
+                grouped[:].rearrange("p (t g i s) -> p t g s i", t=2, i=4, s=PACK),
+                raw.rearrange("p s (g t i) -> p t g s i", t=4, i=4)[:, 2 * u : 2 * u + 2],
             )
             return grouped
 
@@ -166,8 +164,8 @@ def tile_list_kvt_act_kernel(
                 for a in range(PASSES):
                     nc.tensor.matmul_mx(
                         out=bank[:],
-                        lhsT=wv_mx[a][0][:, nb * P : (nb + 1) * P].bitcast(FP8X4),
-                        lhsT_scale=wv_mx[a][1][:, nb * P : (nb + 1) * P],
+                        lhsT=wv_mx[a][nb // 2][0][:, nb % 2 * P : (nb % 2 + 1) * P].bitcast(FP8X4),
+                        lhsT_scale=wv_mx[a][nb // 2][1][:, nb % 2 * P : (nb % 2 + 1) * P],
                         rhs=tab_codes[h][:, a, :].bitcast(FP4X4),
                         rhs_scale=tab_planes[a][:, h * BANK : (h + 1) * BANK],
                         start=(a == 0),
@@ -182,8 +180,8 @@ def tile_list_kvt_act_kernel(
                 for a in range(PASSES):
                     nc.tensor.matmul_mx(
                         out=bank[:, t, :],
-                        lhsT=wq_mx[a][0][:, t * P : (t + 1) * P].bitcast(FP8X4),
-                        lhsT_scale=wq_mx[a][1][:, t * P : (t + 1) * P],
+                        lhsT=wq_mx[a][t // 2][0][:, t % 2 * P : (t % 2 + 1) * P].bitcast(FP8X4),
+                        lhsT_scale=wq_mx[a][t // 2][1][:, t % 2 * P : (t % 2 + 1) * P],
                         rhs=x_mx[a][0][:, mb * P : (mb + 1) * P].bitcast(FP8X4),
                         rhs_scale=x_mx[a][1][:, mb * P : (mb + 1) * P],
                         start=(a == 0),
@@ -219,21 +217,31 @@ def tile_list_kvt_act_kernel(
                 nc.sync.dma_start(out_0[mb * P : (mb + 1) * P, cols], staged[:, cols])
 
         on_vector, on_scalar = nc.vector.tensor_copy, nc.scalar.copy
-        tab_codes = [part_words(gather_words(0), 0)]
-        x_grouped = [interleave(x_raw[a], "x_grouped%d" % a, on_scalar) for a in range(PASSES)]
+
+        def make_wv(a):
+            grouped = [
+                interleave(wv_raw[a][:, :, u * HALF : (u + 1) * HALF], "wv_grouped%d_%d" % (a, u), on_vector)
+                for u in range(2)
+            ]
+            return [quantize(grouped[u], "wv%d_%d" % (a, u)) for u in range(2)]
+
+        def make_wq(a):
+            grouped = [interleave_wq(wq_raw[a][:], u, "wq_grouped%d_%d" % (a, u), on_vector) for u in range(2)]
+            return [quantize(grouped[u], "wq%d_%d" % (a, u)) for u in range(2)]
+
+        picked_first = gather_words(0)
+        deal_wk_scales()
+        tab_codes = [part_words(picked_first, 0)]
+        x_grouped = [interleave(x_raw[a][:], "x_grouped%d" % a, on_scalar) for a in range(PASSES)]
         ka_grouped = [keys(tab_codes[0], 0)]
         tab_codes.append(part_words(gather_words(1), 1))
         ka_grouped.append(keys(tab_codes[1], 1))
         x_mx = [quantize(x_grouped[a], "x%d" % a) for a in range(PASSES)]
-        wv_grouped = [interleave(wv_raw[a], "wv_grouped%d" % a, on_vector) for a in range(PASSES)]
-        wv_mx = [quantize(wv_grouped[a], "wv%d" % a) for a in range(PASSES)]
-        ka_mx = [quantize(ka_grouped[0], "ka0")]
+        wv_mx = [make_wv(a) for a in range(PASSES)]
+        ka_mx = [quantize(ka_grouped[h], "ka%d" % h, "wv_grouped1_%d" % h) for h in range(HALVES)]
         for nb in range(N // P):
             values(nb)
-        wq_grouped0 = interleave_wq(wq_raw[0], "wq_grouped0", on_vector)
-        ka_mx.append(quantize(ka_grouped[1], "ka1"))
-        wq_mx = [quantize(wq_grouped0, "wq0")]
-        wq_mx.append(quantize(interleave_wq(wq_raw[1], "wq_grouped1", on_vector), "wq1"))
+        wq_mx = [make_wq(a) for a in range(PASSES)]
         qa_grouped = [queries(mb) for mb in range(M // P)]
         qa_mx = [quantize(qa_grouped[mb], "qa%d" % mb) for mb in range(M // P)]
         for mb in range(M // P):

@@ -46,7 +46,7 @@ def tile_list_kvt_act_kernel(
 
         scale_win = held([P, T // 4], I32, "scale_win")
         nc.vector.memset(scale_win[:], 0)
-        wk_scale_raw = held([P, PASSES, R // 4], I32, "wk_scale_raw")
+        wk_scale_raw = shared.tile([P, PASSES, R // 4], I32, name="wk_scale_raw", tag="picked1", align_bytes=64)
         nc.vector.memset(wk_scale_raw[:], 0)
         moved_plane = held([P, J // 4], I32, "moved_plane")
         nc.vector.memset(moved_plane[:], 0)
@@ -61,20 +61,21 @@ def tile_list_kvt_act_kernel(
         word_win = held([P, T], I32, "word_win")
         nc.sync.dma_start(word_win[:], tab_words[0].rearrange("p t b -> p (t b)").bitcast(I32))
 
+        def load_pass(src, a, name):
+            raw = shared.tile([P, PACK, src.shape[1]], F32, name=name + "_raw", tag=name, align_bytes=64)
+            rows = src[a * K_PASS : (a + 1) * K_PASS, :]
+            nc.sync.dma_start(raw[:], rows.rearrange("(p s) w -> p s w", s=PACK))
+            return raw
+
+        x_raw = [load_pass(x, 0, "x_raw0")]
         for q in range(4):
             nc.sync.dma_start(
                 wk_scale_raw[32 * q : 32 * q + 4, :, :],
                 wk_scales[:, 4 * q : 4 * q + 4, :].rearrange("a r c -> r a c").bitcast(I32),
             )
 
-        def load_pass(src, a, name):
-            raw = held([P, PACK, src.shape[1]], F32, name)
-            rows = src[a * K_PASS : (a + 1) * K_PASS, :]
-            nc.sync.dma_start(raw[:], rows.rearrange("(p s) w -> p s w", s=PACK))
-            return raw
-
-        x_raw = [load_pass(x, a, "x_raw%d" % a) for a in range(PASSES)]
         wv_raw = [load_pass(wv, a, "wv_raw%d" % a) for a in range(PASSES)]
+        x_raw.append(load_pass(x, 1, "x_raw1"))
         wq_raw = [load_pass(wq, a, "wq_raw%d" % a) for a in range(PASSES)]
 
         picked_plane = held([P, J], U8, "picked_plane")
@@ -114,7 +115,7 @@ def tile_list_kvt_act_kernel(
             return grouped
 
         def interleave_wq(raw, u, name, engine_copy):
-            grouped = held([P, PACK * HALF], BF16, name)
+            grouped = shared.tile([P, PACK * HALF], BF16, name=name, tag=name, align_bytes=64)
             engine_copy(
                 grouped[:].rearrange("p (t g i s) -> p t g s i", t=2, i=4, s=PACK),
                 raw.rearrange("p s (g t i) -> p t g s i", t=4, i=4)[:, 2 * u : 2 * u + 2],
@@ -122,7 +123,7 @@ def tile_list_kvt_act_kernel(
             return grouped
 
         def gather_words(h):
-            picked = held([P, BANK], U32, "picked%d" % h)
+            picked = shared.tile([P, BANK], U32, name="picked%d" % h, tag="picked%d" % h, align_bytes=64)
             cols = slice(h * BANK // 16, (h + 1) * BANK // 16)
             nc.vector.tensor_copy(picked[:], word_win[:].bitcast(U32).indirect(offsets[:, cols]))
             return picked
@@ -158,14 +159,14 @@ def tile_list_kvt_act_kernel(
             return grouped
 
         def values(nb):
-            staged = held([P, J], F32, "vv_staged%d" % nb)
+            staged = shared.tile([P, J], F32, name="vv_staged%d" % nb, tag="vv_staged%d" % nb, align_bytes=64)
             for h in range(HALVES):
                 bank = psum.tile([P, BANK], F32, name="v_bank", tag="bank")
                 for a in range(PASSES):
                     nc.tensor.matmul_mx(
                         out=bank[:],
-                        lhsT=wv_mx[a][nb // 2][0][:, nb % 2 * P : (nb % 2 + 1) * P].bitcast(FP8X4),
-                        lhsT_scale=wv_mx[a][nb // 2][1][:, nb % 2 * P : (nb % 2 + 1) * P],
+                        lhsT=wv_mx[a, nb // 2][0][:, nb % 2 * P : (nb % 2 + 1) * P].bitcast(FP8X4),
+                        lhsT_scale=wv_mx[a, nb // 2][1][:, nb % 2 * P : (nb % 2 + 1) * P],
                         rhs=tab_codes[h][:, a, :].bitcast(FP4X4),
                         rhs_scale=tab_planes[a][:, h * BANK : (h + 1) * BANK],
                         start=(a == 0),
@@ -182,8 +183,8 @@ def tile_list_kvt_act_kernel(
                         out=bank[:, t, :],
                         lhsT=wq_mx[a][t // 2][0][:, t % 2 * P : (t % 2 + 1) * P].bitcast(FP8X4),
                         lhsT_scale=wq_mx[a][t // 2][1][:, t % 2 * P : (t % 2 + 1) * P],
-                        rhs=x_mx[a][0][:, mb * P : (mb + 1) * P].bitcast(FP8X4),
-                        rhs_scale=x_mx[a][1][:, mb * P : (mb + 1) * P],
+                        rhs=x_mx[a][mb][0][:].bitcast(FP8X4),
+                        rhs_scale=x_mx[a][mb][1][:],
                         start=(a == 0),
                         stop=(a == PASSES - 1),
                     )
@@ -218,30 +219,46 @@ def tile_list_kvt_act_kernel(
 
         on_vector, on_scalar = nc.vector.tensor_copy, nc.scalar.copy
 
-        def make_wv(a):
-            grouped = [
+        def group_wv(a):
+            return [
                 interleave(wv_raw[a][:, :, u * HALF : (u + 1) * HALF], "wv_grouped%d_%d" % (a, u), on_vector)
                 for u in range(2)
             ]
-            return [quantize(grouped[u], "wv%d_%d" % (a, u)) for u in range(2)]
 
-        def make_wq(a):
-            grouped = [interleave_wq(wq_raw[a][:], u, "wq_grouped%d_%d" % (a, u), on_vector) for u in range(2)]
+        def make_wq(a, copies):
+            grouped = [interleave_wq(wq_raw[a][:], u, "wq_grouped%d_%d" % (a, u), copies[u]) for u in range(2)]
             return [quantize(grouped[u], "wq%d_%d" % (a, u)) for u in range(2)]
 
-        picked_first = gather_words(0)
+        def group_x(a):
+            return [
+                interleave(x_raw[a][:, :, mb * P : (mb + 1) * P], "x_grouped%d_%d" % (a, mb), on_scalar)
+                for mb in range(M // P)
+            ]
+
+        def quantize_x(grouped, a, tags):
+            return [quantize(grouped[mb], "x%d_%d" % (a, mb), tags[mb]) for mb in range(M // P)]
+
+        tab_codes = [part_words(gather_words(0), 0)]
         deal_wk_scales()
-        tab_codes = [part_words(picked_first, 0)]
-        x_grouped = [interleave(x_raw[a][:], "x_grouped%d" % a, on_scalar) for a in range(PASSES)]
+        x_grouped = [group_x(0)]
         ka_grouped = [keys(tab_codes[0], 0)]
         tab_codes.append(part_words(gather_words(1), 1))
         ka_grouped.append(keys(tab_codes[1], 1))
-        x_mx = [quantize(x_grouped[a], "x%d" % a) for a in range(PASSES)]
-        wv_mx = [make_wv(a) for a in range(PASSES)]
-        ka_mx = [quantize(ka_grouped[h], "ka%d" % h, "wv_grouped1_%d" % h) for h in range(HALVES)]
+        x_grouped.append(group_x(1))
+        wv_grouped = [group_wv(0)]
+        wv_mx = {(0, 0): quantize(wv_grouped[0][0], "wv0_0")}
+        x_mx = [quantize_x(x_grouped[0], 0, ["wv_raw0", "wv_grouped0_0"])]
+        wv_grouped.append(group_wv(1))
+        wv_mx[1, 0] = quantize(wv_grouped[1][0], "wv1_0")
+        wv_mx[0, 1] = quantize(wv_grouped[0][1], "wv0_1", "wv_raw1")
+        wv_mx[1, 1] = quantize(wv_grouped[1][1], "wv1_1")
+        ka_mx = [quantize(ka_grouped[0], "ka0", "wv_grouped1_0")]
         for nb in range(N // P):
             values(nb)
-        wq_mx = [make_wq(a) for a in range(PASSES)]
+        wq_mx = [make_wq(0, [on_vector, on_vector])]
+        x_mx.append(quantize_x(x_grouped[1], 1, ["wq_grouped0_0", "wq_grouped0_1"]))
+        ka_mx.append(quantize(ka_grouped[1], "ka1", "wq_raw0"))
+        wq_mx.append(make_wq(1, [on_vector, on_vector]))
         qa_grouped = [queries(mb) for mb in range(M // P)]
         qa_mx = [quantize(qa_grouped[mb], "qa%d" % mb) for mb in range(M // P)]
         for mb in range(M // P):

@@ -26,6 +26,7 @@ BANK = 512
 HALVES = J // BANK
 SHIFT = 16
 HALF = 256
+LEAD = 1024
 SCORE_SCALE = 0.03125
 
 
@@ -51,15 +52,17 @@ def tile_list_kvt_act_kernel(
         moved_plane = held([P, J // 4], I32, "moved_plane")
         nc.vector.memset(moved_plane[:], 0)
 
-        wk_raw = held([P, PASSES, R], I32, "wk_raw")
-        nc.sync.dma_start(wk_raw[:], wk_words.rearrange("a p r i -> p a (r i)").bitcast(I32))
+        word_win = held([P, T], I32, "word_win")
+        table = tab_words[0].rearrange("p t b -> p (t b)").bitcast(I32)
+        nc.sync.dma_start(word_win[:, 0:LEAD], table[:, 0:LEAD])
 
         scale_rows = tab_scales.rearrange("a (q e) t -> e q a t", e=4).bitcast(I32)
         for e in range(4):
             nc.sync.dma_start(scale_win[e:P:SHIFT, :], scale_rows[e])
 
-        word_win = held([P, T], I32, "word_win")
-        nc.sync.dma_start(word_win[:], tab_words[0].rearrange("p t b -> p (t b)").bitcast(I32))
+        nc.sync.dma_start(word_win[:, LEAD:T], table[:, LEAD:T])
+        wk_raw = shared.tile([P, PASSES, R], I32, name="wk_raw", tag="wk_raw", align_bytes=64)
+        nc.sync.dma_start(wk_raw[:], wk_words.rearrange("a p r i -> p a (r i)").bitcast(I32))
 
         def load_pass(src, a, name):
             raw = shared.tile([P, PACK, src.shape[1]], F32, name=name + "_raw", tag=name, align_bytes=64)
@@ -84,10 +87,13 @@ def tile_list_kvt_act_kernel(
         tab_planes = [picked_plane[:], moved_plane[:].bitcast(U8)]
 
         wk_codes = held([P, PASSES, R], I32, "wk_codes")
-        nc.vector.tensor_copy(
-            wk_codes[:].rearrange("p a (t g i) -> p a t g i", t=4, i=4),
-            wk_raw[:].rearrange("p a (g t i) -> p a t g i", t=4, i=4),
-        )
+
+        def deal_wk_words():
+            nc.vector.tensor_copy(
+                wk_codes[:].rearrange("p a (t g i) -> p a t g i", t=4, i=4),
+                wk_raw[:].rearrange("p a (g t i) -> p a t g i", t=4, i=4),
+            )
+
         wk_plane = held([P, PASSES, R // 4], I32, "wk_plane")
 
         def deal_wk_scales():
@@ -128,8 +134,8 @@ def tile_list_kvt_act_kernel(
             nc.vector.tensor_copy(picked[:], word_win[:].bitcast(U32).indirect(offsets[:, cols]))
             return picked
 
-        def part_words(picked, h):
-            codes = held([P, PASSES, 2 * BANK], U8, "tab_codes%d" % h)
+        def part_words(picked, h, tag):
+            codes = shared.tile([P, PASSES, 2 * BANK], U8, name="tab_codes%d" % h, tag=tag, align_bytes=64)
             nc.vector.tensor_copy(
                 codes[:].bitcast(U16),
                 picked[:].bitcast(U16).rearrange("p (j d) -> p d j", d=PASSES),
@@ -238,11 +244,13 @@ def tile_list_kvt_act_kernel(
         def quantize_x(grouped, a, tags):
             return [quantize(grouped[mb], "x%d_%d" % (a, mb), tags[mb]) for mb in range(M // P)]
 
-        tab_codes = [part_words(gather_words(0), 0)]
+        picked_first = gather_words(0)
+        deal_wk_words()
+        tab_codes = [part_words(picked_first, 0, "wk_raw")]
         deal_wk_scales()
         x_grouped = [group_x(0)]
         ka_grouped = [keys(tab_codes[0], 0)]
-        tab_codes.append(part_words(gather_words(1), 1))
+        tab_codes.append(part_words(gather_words(1), 1, "tab_codes1"))
         ka_grouped.append(keys(tab_codes[1], 1))
         x_grouped.append(group_x(1))
         wv_grouped = [group_wv(0)]
@@ -255,9 +263,9 @@ def tile_list_kvt_act_kernel(
         ka_mx = [quantize(ka_grouped[0], "ka0", "wv_grouped1_0")]
         for nb in range(N // P):
             values(nb)
+        ka_mx.append(quantize(ka_grouped[1], "ka1", "wv_grouped1_1"))
         wq_mx = [make_wq(0, [on_vector, on_vector])]
-        x_mx.append(quantize_x(x_grouped[1], 1, ["wq_grouped0_0", "wq_grouped0_1"]))
-        ka_mx.append(quantize(ka_grouped[1], "ka1", "wq_raw0"))
+        x_mx.append(quantize_x(x_grouped[1], 1, ["wq_raw0", "wq_grouped0_0"]))
         wq_mx.append(make_wq(1, [on_vector, on_vector]))
         qa_grouped = [queries(mb) for mb in range(M // P)]
         qa_mx = [quantize(qa_grouped[mb], "qa%d" % mb) for mb in range(M // P)]

@@ -45,10 +45,15 @@ def tile_list_kvt_act_kernel(
         offsets = keep.tile([P, J // 16], U16, name="offsets")
         nc.sync.dma_start(offsets[:], offs)
 
-        scale_win = held([P, T // 4], I32, "scale_win")
+        scale_win = shared.tile([P, T // 4], I32, name="scale_win", tag="scale_win", align_bytes=64)
         nc.vector.memset(scale_win[:], 0)
-        wk_scale_raw = shared.tile([P, PASSES, R // 4], I32, name="wk_scale_raw", tag="picked1", align_bytes=64)
-        nc.vector.memset(wk_scale_raw[:], 0)
+        wk_scale_raw = held([P, PASSES, R // 4], I32, "wk_scale_raw")
+        nc.gpsimd.memset(wk_scale_raw[:], 0)
+        for q in range(4):
+            nc.gpsimd.dma_start(
+                wk_scale_raw[32 * q : 32 * q + 4, :, :],
+                wk_scales[:, 4 * q : 4 * q + 4, :].rearrange("a r c -> r a c").bitcast(I32),
+            )
         moved_plane = held([P, J // 4], I32, "moved_plane")
         nc.vector.memset(moved_plane[:], 0)
 
@@ -71,12 +76,6 @@ def tile_list_kvt_act_kernel(
             return raw
 
         x_raw = [load_pass(x, 0, "x_raw0")]
-        for q in range(4):
-            nc.sync.dma_start(
-                wk_scale_raw[32 * q : 32 * q + 4, :, :],
-                wk_scales[:, 4 * q : 4 * q + 4, :].rearrange("a r c -> r a c").bitcast(I32),
-            )
-
         wv_raw = [load_pass(wv, a, "wv_raw%d" % a) for a in range(PASSES)]
         x_raw.append(load_pass(x, 1, "x_raw1"))
         wq_raw = [load_pass(wq, a, "wq_raw%d" % a) for a in range(PASSES)]
@@ -94,7 +93,7 @@ def tile_list_kvt_act_kernel(
                 wk_raw[:].rearrange("p a (g t i) -> p a t g i", t=4, i=4),
             )
 
-        wk_plane = held([P, PASSES, R // 4], I32, "wk_plane")
+        wk_plane = shared.tile([P, PASSES, R // 4], I32, name="wk_plane", tag="scale_win", align_bytes=64)
 
         def deal_wk_scales():
             nc.vector.tensor_copy(
@@ -128,8 +127,8 @@ def tile_list_kvt_act_kernel(
             )
             return grouped
 
-        def gather_words(h):
-            picked = shared.tile([P, BANK], U32, name="picked%d" % h, tag="picked%d" % h, align_bytes=64)
+        def gather_words(h, tag):
+            picked = shared.tile([P, BANK], U32, name="picked%d" % h, tag=tag, align_bytes=64)
             cols = slice(h * BANK // 16, (h + 1) * BANK // 16)
             nc.vector.tensor_copy(picked[:], word_win[:].bitcast(U32).indirect(offsets[:, cols]))
             return picked
@@ -244,13 +243,12 @@ def tile_list_kvt_act_kernel(
         def quantize_x(grouped, a, tags):
             return [quantize(grouped[mb], "x%d_%d" % (a, mb), tags[mb]) for mb in range(M // P)]
 
-        picked_first = gather_words(0)
-        deal_wk_words()
-        tab_codes = [part_words(picked_first, 0, "wk_raw")]
         deal_wk_scales()
+        tab_codes = [part_words(gather_words(0, "picked0"), 0, "tab_codes0")]
+        deal_wk_words()
         x_grouped = [group_x(0)]
         ka_grouped = [keys(tab_codes[0], 0)]
-        tab_codes.append(part_words(gather_words(1), 1, "tab_codes1"))
+        tab_codes.append(part_words(gather_words(1, "wk_raw"), 1, "tab_codes1"))
         ka_grouped.append(keys(tab_codes[1], 1))
         x_grouped.append(group_x(1))
         wv_grouped = [group_wv(0)]
@@ -263,9 +261,9 @@ def tile_list_kvt_act_kernel(
         ka_mx = [quantize(ka_grouped[0], "ka0", "wv_grouped1_0")]
         for nb in range(N // P):
             values(nb)
-        ka_mx.append(quantize(ka_grouped[1], "ka1", "wv_grouped1_1"))
         wq_mx = [make_wq(0, [on_vector, on_vector])]
-        x_mx.append(quantize_x(x_grouped[1], 1, ["wq_raw0", "wq_grouped0_0"]))
+        ka_mx.append(quantize(ka_grouped[1], "ka1", "wq_raw0"))
+        x_mx.append(quantize_x(x_grouped[1], 1, ["wq_grouped0_0", "wq_grouped0_1"]))
         wq_mx.append(make_wq(1, [on_vector, on_vector]))
         qa_grouped = [queries(mb) for mb in range(M // P)]
         qa_mx = [quantize(qa_grouped[mb], "qa%d" % mb) for mb in range(M // P)]

@@ -37,7 +37,7 @@ def tile_list_kvt_act_kernel(
     with ExitStack() as ctx:
         keep = ctx.enter_context(tc.tile_pool(name="keep", bufs=1))
         shared = ctx.enter_context(tc.tile_pool(name="shared", bufs=1))
-        psum = ctx.enter_context(tc.psum_pool(name="psum", bufs=8))
+        psum = ctx.enter_context(tc.psum_pool(name="psum", bufs=4))
 
         def held(shape, dtype, name):
             return keep.tile(shape, dtype, name=name, align_bytes=64)
@@ -54,8 +54,9 @@ def tile_list_kvt_act_kernel(
                 wk_scale_raw[32 * q : 32 * q + 4, :, :],
                 wk_scales[:, 4 * q : 4 * q + 4, :].rearrange("a r c -> r a c").bitcast(I32),
             )
-        moved_plane = held([P, J // 4], I32, "moved_plane")
-        nc.vector.memset(moved_plane[:], 0)
+        moved_planes = [held([P, BANK // 4], I32, "moved_plane%d" % h) for h in range(HALVES)]
+        for moved in moved_planes:
+            nc.vector.memset(moved[:], 0)
 
         word_win = held([P, T], I32, "word_win")
         table = tab_words[0].rearrange("p t b -> p (t b)").bitcast(I32)
@@ -77,13 +78,16 @@ def tile_list_kvt_act_kernel(
 
         x_raw = [load_pass(x, 0, "x_raw0")]
         wv_raw = [load_pass(wv, a, "wv_raw%d" % a) for a in range(PASSES)]
-        x_raw.append(load_pass(x, 1, "x_raw1"))
         wq_raw = [load_pass(wq, a, "wq_raw%d" % a) for a in range(PASSES)]
+        x_raw.append(load_pass(x, 1, "x_raw1"))
 
-        picked_plane = held([P, J], U8, "picked_plane")
-        nc.vector.tensor_copy(picked_plane[:], scale_win[:].bitcast(U8).indirect(offsets[:]))
-        nc.scalar.dma_start(moved_plane[0 : P - SHIFT, :], picked_plane[SHIFT:P, :].bitcast(I32))
-        tab_planes = [picked_plane[:], moved_plane[:].bitcast(U8)]
+        tab_planes = []
+        for h in range(HALVES):
+            picked_plane = held([P, BANK], U8, "picked_plane%d" % h)
+            cols = slice(h * BANK // 16, (h + 1) * BANK // 16)
+            nc.vector.tensor_copy(picked_plane[:], scale_win[:].bitcast(U8).indirect(offsets[:, cols]))
+            nc.scalar.dma_start(moved_planes[h][0 : P - SHIFT, :], picked_plane[SHIFT:P, :].bitcast(I32))
+            tab_planes.append([picked_plane[:], moved_planes[h][:].bitcast(U8)])
 
         wk_codes = held([P, PASSES, R], I32, "wk_codes")
 
@@ -152,7 +156,7 @@ def tile_list_kvt_act_kernel(
                             lhsT=wk_codes[:, a, t * P : (t + 1) * P].bitcast(FP8X4),
                             lhsT_scale=wk_plane[:, a, :].bitcast(U8)[:, t * P : (t + 1) * P],
                             rhs=codes[:, a, 2 * b * P : 2 * (b + 1) * P].bitcast(FP4X4),
-                            rhs_scale=tab_planes[a][:, h * BANK + b * P : h * BANK + (b + 1) * P],
+                            rhs_scale=tab_planes[h][a][:, b * P : (b + 1) * P],
                             start=(a == 0),
                             stop=(a == PASSES - 1),
                         )
@@ -163,8 +167,8 @@ def tile_list_kvt_act_kernel(
                 )
             return grouped
 
-        def values(nb):
-            staged = shared.tile([P, J], F32, name="vv_staged%d" % nb, tag="vv_staged%d" % nb, align_bytes=64)
+        def values(nb, tag):
+            staged = shared.tile([P, J], F32, name="vv_staged%d" % nb, tag=tag, align_bytes=64)
             for h in range(HALVES):
                 bank = psum.tile([P, BANK], F32, name="v_bank", tag="bank")
                 for a in range(PASSES):
@@ -173,7 +177,7 @@ def tile_list_kvt_act_kernel(
                         lhsT=wv_mx[a, nb // 2][0][:, nb % 2 * P : (nb % 2 + 1) * P].bitcast(FP8X4),
                         lhsT_scale=wv_mx[a, nb // 2][1][:, nb % 2 * P : (nb % 2 + 1) * P],
                         rhs=tab_codes[h][:, a, :].bitcast(FP4X4),
-                        rhs_scale=tab_planes[a][:, h * BANK : (h + 1) * BANK],
+                        rhs_scale=tab_planes[h][a],
                         start=(a == 0),
                         stop=(a == PASSES - 1),
                     )
@@ -182,16 +186,16 @@ def tile_list_kvt_act_kernel(
 
         def queries(mb):
             bank = psum.tile([P, PACK, P], F32, name="q_bank", tag="bank")
-            for t in range(PACK):
-                for a in range(PASSES):
+            for a in range(PASSES):
+                for t in range(PACK):
                     nc.tensor.matmul_mx(
                         out=bank[:, t, :],
                         lhsT=wq_mx[a][t // 2][0][:, t % 2 * P : (t % 2 + 1) * P].bitcast(FP8X4),
                         lhsT_scale=wq_mx[a][t // 2][1][:, t % 2 * P : (t % 2 + 1) * P],
                         rhs=x_mx[a][mb][0][:].bitcast(FP8X4),
                         rhs_scale=x_mx[a][mb][1][:],
-                        start=(a == 0),
-                        stop=(a == PASSES - 1),
+                        start=(a == 0 and t == 0),
+                        stop=(a == PASSES - 1 and t == PACK - 1),
                     )
             grouped = held([P, PACK * P], BF16, "qa_grouped%d" % mb)
             out = grouped[:].rearrange("p (m t) -> p m t", t=PACK)
@@ -250,7 +254,6 @@ def tile_list_kvt_act_kernel(
         ka_grouped = [keys(tab_codes[0], 0)]
         tab_codes.append(part_words(gather_words(1, "wk_raw"), 1, "tab_codes1"))
         ka_grouped.append(keys(tab_codes[1], 1))
-        x_grouped.append(group_x(1))
         wv_grouped = [group_wv(0)]
         wv_mx = {(0, 0): quantize(wv_grouped[0][0], "wv0_0")}
         x_mx = [quantize_x(x_grouped[0], 0, ["wv_raw0", "wv_grouped0_0"])]
@@ -259,13 +262,15 @@ def tile_list_kvt_act_kernel(
         wv_mx[0, 1] = quantize(wv_grouped[0][1], "wv0_1", "wv_raw1")
         wv_mx[1, 1] = quantize(wv_grouped[1][1], "wv1_1")
         ka_mx = [quantize(ka_grouped[0], "ka0", "wv_grouped1_0")]
-        for nb in range(N // P):
-            values(nb)
+        for nb in range(3):
+            values(nb, "vv_staged%d" % nb)
         wq_mx = [make_wq(0, [on_vector, on_vector])]
         ka_mx.append(quantize(ka_grouped[1], "ka1", "wq_raw0"))
-        x_mx.append(quantize_x(x_grouped[1], 1, ["wq_grouped0_0", "wq_grouped0_1"]))
         wq_mx.append(make_wq(1, [on_vector, on_vector]))
+        x_grouped.append(group_x(1))
+        x_mx.append(quantize_x(x_grouped[1], 1, [None, None]))
         qa_grouped = [queries(mb) for mb in range(M // P)]
+        values(3, "x_raw1")
         qa_mx = [quantize(qa_grouped[mb], "qa%d" % mb) for mb in range(M // P)]
         for mb in range(M // P):
             scores(qa_mx[mb], mb)

@@ -38,6 +38,7 @@ def tile_list_kvt_act_kernel(
         keep = ctx.enter_context(tc.tile_pool(name="keep", bufs=1))
         shared = ctx.enter_context(tc.tile_pool(name="shared", bufs=1))
         psum = ctx.enter_context(tc.psum_pool(name="psum", bufs=4))
+        narrow = ctx.enter_context(tc.psum_pool(name="narrow", bufs=4))
 
         def held(shape, dtype, name):
             return keep.tile(shape, dtype, name=name, align_bytes=64)
@@ -97,13 +98,13 @@ def tile_list_kvt_act_kernel(
                 wk_raw[:].rearrange("p a (g t i) -> p a t g i", t=4, i=4),
             )
 
-        wk_plane = shared.tile([P, PASSES, R // 4], I32, name="wk_plane", tag="scale_win", align_bytes=64)
-
         def deal_wk_scales():
+            wk_plane = shared.tile([P, PASSES, R // 4], I32, name="wk_plane", tag="picked0", align_bytes=64)
             nc.vector.tensor_copy(
                 wk_plane[:].rearrange("p a (t g) -> p a t g", t=4),
                 wk_scale_raw[:].rearrange("p a (g t) -> p a t g", t=4),
             )
+            return wk_plane
 
         def quantize(grouped, name, tag=None):
             width = grouped.shape[1] // PACK
@@ -149,16 +150,16 @@ def tile_list_kvt_act_kernel(
             grouped = held([P, PACK * BANK], BF16, "ka_grouped%d" % h)
             for b in range(BANK // P):
                 bank = psum.tile([P, PACK, P], F32, name="k_bank", tag="bank")
-                for t in range(PACK):
-                    for a in range(PASSES):
+                for a in range(PASSES):
+                    for t in range(PACK):
                         nc.tensor.matmul_mx(
                             out=bank[:, t, :],
                             lhsT=wk_codes[:, a, t * P : (t + 1) * P].bitcast(FP8X4),
                             lhsT_scale=wk_plane[:, a, :].bitcast(U8)[:, t * P : (t + 1) * P],
                             rhs=codes[:, a, 2 * b * P : 2 * (b + 1) * P].bitcast(FP4X4),
                             rhs_scale=tab_planes[h][a][:, b * P : (b + 1) * P],
-                            start=(a == 0),
-                            stop=(a == PASSES - 1),
+                            start=(a == 0 and t == 0),
+                            stop=(a == PASSES - 1 and t == PACK - 1),
                         )
                 nc.scalar.activation(
                     grouped[:, b * BANK : (b + 1) * BANK].rearrange("p (j t) -> p j t", t=PACK),
@@ -209,20 +210,22 @@ def tile_list_kvt_act_kernel(
         def scores(qa, mb):
             staged = held([P, J], F32, "sc_staged%d" % mb)
             for h in range(HALVES):
-                bank = psum.tile([P, BANK], F32, name="s_bank", tag="bank")
-                nc.tensor.matmul_mx(
-                    out=bank[:],
-                    lhsT=qa[0][:].bitcast(FP8X4),
-                    lhsT_scale=qa[1][:],
-                    rhs=ka_mx[h][0][:].bitcast(FP8X4),
-                    rhs_scale=ka_mx[h][1][:],
-                    start=True,
-                    stop=True,
-                )
-                if h == 0:
-                    nc.scalar.activation(staged[:, 0:BANK], bank[:], COPY, scale=SCORE_SCALE)
-                else:
-                    nc.vector.tensor_scalar(staged[:, BANK:J], bank[:], SCORE_SCALE, None, MULT)
+                for u in range(2):
+                    bank = narrow.tile([P, HALF], F32, name="s_bank", tag="s_bank")
+                    nc.tensor.matmul_mx(
+                        out=bank[:],
+                        lhsT=qa[0][:].bitcast(FP8X4),
+                        lhsT_scale=qa[1][:],
+                        rhs=ka_mx[h][0][:, u * HALF : (u + 1) * HALF].bitcast(FP8X4),
+                        rhs_scale=ka_mx[h][1][:, u * HALF : (u + 1) * HALF],
+                        start=True,
+                        stop=True,
+                    )
+                    part = staged[:, h * BANK + u * HALF : h * BANK + (u + 1) * HALF]
+                    if u == 0:
+                        nc.scalar.activation(part, bank[:], COPY, scale=SCORE_SCALE)
+                    else:
+                        nc.vector.tensor_scalar(part, bank[:], SCORE_SCALE, None, MULT)
                 cols = slice(h * BANK, (h + 1) * BANK)
                 nc.sync.dma_start(out_0[mb * P : (mb + 1) * P, cols], staged[:, cols])
 
@@ -238,25 +241,27 @@ def tile_list_kvt_act_kernel(
             grouped = [interleave_wq(wq_raw[a][:], u, "wq_grouped%d_%d" % (a, u), copies[u]) for u in range(2)]
             return [quantize(grouped[u], "wq%d_%d" % (a, u)) for u in range(2)]
 
-        def group_x(a):
+        def group_x(a, copies):
             return [
-                interleave(x_raw[a][:, :, mb * P : (mb + 1) * P], "x_grouped%d_%d" % (a, mb), on_scalar)
+                interleave(x_raw[a][:, :, mb * P : (mb + 1) * P], "x_grouped%d_%d" % (a, mb), copies[mb])
                 for mb in range(M // P)
             ]
 
         def quantize_x(grouped, a, tags):
             return [quantize(grouped[mb], "x%d_%d" % (a, mb), tags[mb]) for mb in range(M // P)]
 
-        deal_wk_scales()
         tab_codes = [part_words(gather_words(0, "picked0"), 0, "tab_codes0")]
         deal_wk_words()
-        x_grouped = [group_x(0)]
+        wk_plane = deal_wk_scales()
+        x_first = interleave(x_raw[0][:], "x_grouped0", on_scalar)
+        x_grouped = [None]
         ka_grouped = [keys(tab_codes[0], 0)]
         tab_codes.append(part_words(gather_words(1, "wk_raw"), 1, "tab_codes1"))
         ka_grouped.append(keys(tab_codes[1], 1))
         wv_grouped = [group_wv(0)]
         wv_mx = {(0, 0): quantize(wv_grouped[0][0], "wv0_0")}
-        x_mx = [quantize_x(x_grouped[0], 0, ["wv_raw0", "wv_grouped0_0"])]
+        x_codes, x_plane = quantize(x_first, "x0", "wv_raw0")
+        x_mx = [[(x_codes[:, mb * P : (mb + 1) * P], x_plane[:, mb * P : (mb + 1) * P]) for mb in range(M // P)]]
         wv_grouped.append(group_wv(1))
         wv_mx[1, 0] = quantize(wv_grouped[1][0], "wv1_0")
         wv_mx[0, 1] = quantize(wv_grouped[0][1], "wv0_1", "wv_raw1")
@@ -267,7 +272,7 @@ def tile_list_kvt_act_kernel(
         wq_mx = [make_wq(0, [on_vector, on_vector])]
         ka_mx.append(quantize(ka_grouped[1], "ka1", "wq_raw0"))
         wq_mx.append(make_wq(1, [on_vector, on_vector]))
-        x_grouped.append(group_x(1))
+        x_grouped.append(group_x(1, [on_scalar, on_scalar]))
         x_mx.append(quantize_x(x_grouped[1], 1, [None, None]))
         qa_grouped = [queries(mb) for mb in range(M // P)]
         values(3, "x_raw1")

@@ -119,17 +119,17 @@ def tile_list_kvt_act_kernel(
         def interleave(raw, name, engine_copy):
             grouped = shared.tile([P, PACK * raw.shape[2]], BF16, name=name, tag=name, align_bytes=64)
             engine_copy(
-                grouped[:].rearrange("p (c i s) -> p c s i", i=4, s=PACK),
-                raw.rearrange("p s (c i) -> p c s i", i=4),
+                grouped[:].rearrange("p (c i s) -> p c s i", i=2, s=PACK),
+                raw.rearrange("p s (c i) -> p c s i", i=2),
             )
             return grouped
 
         def interleave_wq(raw, u, name, engine_copy):
             grouped = shared.tile([P, PACK * HALF], BF16, name=name, tag=name, align_bytes=64)
-            engine_copy(
-                grouped[:].rearrange("p (t g i s) -> p t g s i", t=2, i=4, s=PACK),
-                raw.rearrange("p s (g t i) -> p t g s i", t=4, i=4)[:, 2 * u : 2 * u + 2],
-            )
+            dealt = grouped[:].rearrange("p (t g j i s) -> p t g j s i", t=2, j=2, i=2, s=PACK)
+            source = raw.rearrange("p s (g t j i) -> p t g j s i", t=4, j=2, i=2)
+            for t in range(2):
+                engine_copy(dealt[:, t], source[:, 2 * u + t])
             return grouped
 
         def gather_words(h, tag):

@@ -37,8 +37,8 @@ def tile_list_kvt_act_kernel(
     with ExitStack() as ctx:
         keep = ctx.enter_context(tc.tile_pool(name="keep", bufs=1))
         shared = ctx.enter_context(tc.tile_pool(name="shared", bufs=1))
-        psum = ctx.enter_context(tc.psum_pool(name="psum", bufs=4))
-        narrow = ctx.enter_context(tc.psum_pool(name="narrow", bufs=4))
+        placed = ctx.enter_context(tc.tile_pool(name="placed", bufs=1))
+        psum = ctx.enter_context(tc.psum_pool(name="psum", bufs=8))
 
         def held(shape, dtype, name):
             return keep.tile(shape, dtype, name=name, align_bytes=64)
@@ -71,14 +71,15 @@ def tile_list_kvt_act_kernel(
         wk_raw = shared.tile([P, PASSES, R], I32, name="wk_raw", tag="wk_raw", align_bytes=64)
         nc.sync.dma_start(wk_raw[:], wk_words.rearrange("a p r i -> p a (r i)").bitcast(I32))
 
-        def load_pass(src, a, name):
-            raw = shared.tile([P, PACK, src.shape[1]], F32, name=name + "_raw", tag=name, align_bytes=64)
+        def load_pass(src, a, name, offset=None):
+            pool = shared if offset is None else placed
+            raw = pool.tile([P, PACK, src.shape[1]], F32, name=name + "_raw", tag=name, align_bytes=64, offset=offset)
             rows = src[a * K_PASS : (a + 1) * K_PASS, :]
             nc.sync.dma_start(raw[:], rows.rearrange("(p s) w -> p s w", s=PACK))
             return raw
 
         x_raw = [load_pass(x, 0, "x_raw0")]
-        wv_raw = [load_pass(wv, a, "wv_raw%d" % a) for a in range(PASSES)]
+        wv_raw = [load_pass(wv, 0, "wv_raw0", 2 * BANK), load_pass(wv, 1, "wv_raw1")]
         wq_raw = [load_pass(wq, a, "wq_raw%d" % a) for a in range(PASSES)]
         x_raw.append(load_pass(x, 1, "x_raw1"))
 
@@ -116,6 +117,14 @@ def tile_list_kvt_act_kernel(
             nc.vector.quantize_mx(out=codes[:].bitcast(FP8X4), scales=plane[:], in_=grouped[:])
             return codes, plane
 
+        def quantize_keys(grouped, name, tag):
+            codes = shared.tile([P, BANK], U32, name=name + "_codes", tag=tag, align_bytes=64)
+            plane = held([P, BANK], U8, name + "_plane")
+            for b in range(BANK // P):
+                cols = slice(b * P, (b + 1) * P)
+                nc.vector.quantize_mx(out=codes[:, cols].bitcast(FP8X4), scales=plane[:, cols], in_=grouped[b][:])
+            return codes, plane
+
         def interleave(raw, name, engine_copy):
             grouped = shared.tile([P, PACK * raw.shape[2]], BF16, name=name, tag=name, align_bytes=64)
             engine_copy(
@@ -126,10 +135,9 @@ def tile_list_kvt_act_kernel(
 
         def interleave_wq(raw, u, name, engine_copy):
             grouped = shared.tile([P, PACK * HALF], BF16, name=name, tag=name, align_bytes=64)
-            dealt = grouped[:].rearrange("p (t g j i s) -> p t g j s i", t=2, j=2, i=2, s=PACK)
-            source = raw.rearrange("p s (g t j i) -> p t g j s i", t=4, j=2, i=2)
-            for t in range(2):
-                engine_copy(dealt[:, t], source[:, 2 * u + t])
+            dealt = grouped[:].rearrange("p (t g i s) -> p t g s i", t=2, i=4, s=PACK)
+            source = raw.rearrange("p s (g t i) -> p t g s i", t=4, i=4)
+            engine_copy(dealt, source[:, 2 * u : 2 * u + 2])
             return grouped
 
         def gather_words(h, tag):
@@ -147,8 +155,10 @@ def tile_list_kvt_act_kernel(
             return codes
 
         def keys(codes, h):
-            grouped = held([P, PACK * BANK], BF16, "ka_grouped%d" % h)
+            grouped = []
             for b in range(BANK // P):
+                n = h * BANK // P + b
+                grouped.append(placed.tile([P, BANK], BF16, name="ka_grouped%d" % n, align_bytes=64, offset=n * 2 * BANK))
                 bank = psum.tile([P, PACK, P], F32, name="k_bank", tag="bank")
                 for a in range(PASSES):
                     for t in range(PACK):
@@ -162,7 +172,7 @@ def tile_list_kvt_act_kernel(
                             stop=(a == PASSES - 1 and t == PACK - 1),
                         )
                 nc.scalar.activation(
-                    grouped[:, b * BANK : (b + 1) * BANK].rearrange("p (j t) -> p j t", t=PACK),
+                    grouped[b][:].rearrange("p (j t) -> p j t", t=PACK),
                     bank[:].rearrange("p t j -> p j t"),
                     RELU,
                 )
@@ -172,15 +182,15 @@ def tile_list_kvt_act_kernel(
             staged = shared.tile([P, J], F32, name="vv_staged%d" % nb, tag=tag, align_bytes=64)
             for h in range(HALVES):
                 bank = psum.tile([P, BANK], F32, name="v_bank", tag="bank")
-                for a in range(PASSES):
+                for a in reversed(range(PASSES)):
                     nc.tensor.matmul_mx(
                         out=bank[:],
                         lhsT=wv_mx[a, nb // 2][0][:, nb % 2 * P : (nb % 2 + 1) * P].bitcast(FP8X4),
                         lhsT_scale=wv_mx[a, nb // 2][1][:, nb % 2 * P : (nb % 2 + 1) * P],
                         rhs=tab_codes[h][:, a, :].bitcast(FP4X4),
                         rhs_scale=tab_planes[h][a],
-                        start=(a == 0),
-                        stop=(a == PASSES - 1),
+                        start=(a == PASSES - 1),
+                        stop=(a == 0),
                     )
                 nc.scalar.copy(staged[:, h * BANK : (h + 1) * BANK], bank[:])
             nc.sync.dma_start(out_1[nb * P : (nb + 1) * P, :], staged[:])
@@ -211,7 +221,7 @@ def tile_list_kvt_act_kernel(
             staged = held([P, J], F32, "sc_staged%d" % mb)
             for h in range(HALVES):
                 for u in range(2):
-                    bank = narrow.tile([P, HALF], F32, name="s_bank", tag="s_bank")
+                    bank = psum.tile([P, HALF], F32, name="s_bank", tag="bank")
                     nc.tensor.matmul_mx(
                         out=bank[:],
                         lhsT=qa[0][:].bitcast(FP8X4),
@@ -222,7 +232,7 @@ def tile_list_kvt_act_kernel(
                         stop=True,
                     )
                     part = staged[:, h * BANK + u * HALF : h * BANK + (u + 1) * HALF]
-                    if u == 0:
+                    if h == 0:
                         nc.scalar.activation(part, bank[:], COPY, scale=SCORE_SCALE)
                     else:
                         nc.vector.tensor_scalar(part, bank[:], SCORE_SCALE, None, MULT)
@@ -231,51 +241,44 @@ def tile_list_kvt_act_kernel(
 
         on_vector, on_scalar = nc.vector.tensor_copy, nc.scalar.copy
 
-        def group_wv(a):
-            return [
-                interleave(wv_raw[a][:, :, u * HALF : (u + 1) * HALF], "wv_grouped%d_%d" % (a, u), on_vector)
-                for u in range(2)
-            ]
+        def group_wv(a, u, engine_copy):
+            return interleave(wv_raw[a][:, :, u * HALF : (u + 1) * HALF], "wv_grouped%d_%d" % (a, u), engine_copy)
 
-        def make_wq(a, copies):
-            grouped = [interleave_wq(wq_raw[a][:], u, "wq_grouped%d_%d" % (a, u), copies[u]) for u in range(2)]
+        def group_wq(a):
+            return [interleave_wq(wq_raw[a][:], u, "wq_grouped%d_%d" % (a, u), on_vector) for u in range(2)]
+
+        def quantize_wq(grouped, a):
             return [quantize(grouped[u], "wq%d_%d" % (a, u)) for u in range(2)]
 
-        def group_x(a, copies):
-            return [
-                interleave(x_raw[a][:, :, mb * P : (mb + 1) * P], "x_grouped%d_%d" % (a, mb), copies[mb])
-                for mb in range(M // P)
-            ]
-
-        def quantize_x(grouped, a, tags):
-            return [quantize(grouped[mb], "x%d_%d" % (a, mb), tags[mb]) for mb in range(M // P)]
+        def quantize_x(grouped, a, tag=None):
+            codes, plane = quantize(grouped, "x%d" % a, tag)
+            return [(codes[:, mb * P : (mb + 1) * P], plane[:, mb * P : (mb + 1) * P]) for mb in range(M // P)]
 
         tab_codes = [part_words(gather_words(0, "picked0"), 0, "tab_codes0")]
         deal_wk_words()
         wk_plane = deal_wk_scales()
         x_first = interleave(x_raw[0][:], "x_grouped0", on_scalar)
-        x_grouped = [None]
-        ka_grouped = [keys(tab_codes[0], 0)]
         tab_codes.append(part_words(gather_words(1, "wk_raw"), 1, "tab_codes1"))
-        ka_grouped.append(keys(tab_codes[1], 1))
-        wv_grouped = [group_wv(0)]
-        wv_mx = {(0, 0): quantize(wv_grouped[0][0], "wv0_0")}
-        x_codes, x_plane = quantize(x_first, "x0", "wv_raw0")
-        x_mx = [[(x_codes[:, mb * P : (mb + 1) * P], x_plane[:, mb * P : (mb + 1) * P]) for mb in range(M // P)]]
-        wv_grouped.append(group_wv(1))
-        wv_mx[1, 0] = quantize(wv_grouped[1][0], "wv1_0")
-        wv_mx[0, 1] = quantize(wv_grouped[0][1], "wv0_1", "wv_raw1")
-        wv_mx[1, 1] = quantize(wv_grouped[1][1], "wv1_1")
-        ka_mx = [quantize(ka_grouped[0], "ka0", "wv_grouped1_0")]
-        for nb in range(3):
+        wv_grouped = {(0, 0): group_wv(0, 0, on_vector), (0, 1): group_wv(0, 1, on_scalar)}
+        ka_grouped = [keys(tab_codes[h], h) for h in range(HALVES)]
+        x_mx = [quantize_x(x_first, 0)]
+        wv_mx = {(0, u): quantize(wv_grouped[0, u], "wv0_%d" % u) for u in range(2)}
+        for u in range(2):
+            wv_grouped[1, u] = group_wv(1, u, on_vector)
+        for u in range(2):
+            wv_mx[1, u] = quantize(wv_grouped[1, u], "wv1_%d" % u)
+        x_late = interleave(x_raw[1][:, :, P:M], "x_grouped1_1", on_scalar)
+        for nb in range(N // P - 1):
             values(nb, "vv_staged%d" % nb)
-        wq_mx = [make_wq(0, [on_vector, on_vector])]
-        ka_mx.append(quantize(ka_grouped[1], "ka1", "wq_raw0"))
-        wq_mx.append(make_wq(1, [on_vector, on_vector]))
-        x_grouped.append(group_x(1, [on_scalar, on_scalar]))
-        x_mx.append(quantize_x(x_grouped[1], 1, [None, None]))
+        values(N // P - 1, "x_raw1")
+        wq_mx = [quantize_wq(group_wq(0), 0)]
+        wq_last = group_wq(1)
+        x_last = [interleave(x_raw[1][:, :, 0:P], "x_grouped1_0", on_vector), x_late]
+        wq_mx.append(quantize_wq(wq_last, 1))
+        x_mx.append([quantize(x_last[mb], "x1_%d" % mb, "x1_codes%d" % mb) for mb in range(M // P)])
+        ka_mx = [quantize_keys(ka_grouped[0], "ka0", "x_grouped1_0")]
         qa_grouped = [queries(mb) for mb in range(M // P)]
-        values(3, "x_raw1")
         qa_mx = [quantize(qa_grouped[mb], "qa%d" % mb) for mb in range(M // P)]
+        ka_mx.append(quantize_keys(ka_grouped[1], "ka1", "x1_codes0"))
         for mb in range(M // P):
             scores(qa_mx[mb], mb)

@@ -267,18 +267,17 @@ def tile_list_kvt_act_kernel(
             wv_grouped[1, u] = group_wv(1, u, on_vector)
         for u in range(2):
             wv_mx[1, u] = quantize(wv_grouped[1, u], "wv1_%d" % u)
-        x_late = interleave(x_raw[1][:, :, P:M], "x_grouped1_1", on_scalar)
-        for nb in range(N // P - 1):
+        for nb in range(N // P):
             values(nb, "vv_staged%d" % nb)
-        values(N // P - 1, "x_raw1")
         wq_mx = [quantize_wq(group_wq(0), 0)]
         wq_last = group_wq(1)
-        x_last = [interleave(x_raw[1][:, :, 0:P], "x_grouped1_0", on_vector), x_late]
+        x_last = interleave(x_raw[1][:, :, 0:P], "x_grouped1_0", on_vector)
         wq_mx.append(quantize_wq(wq_last, 1))
-        x_mx.append([quantize(x_last[mb], "x1_%d" % mb, "x1_codes%d" % mb) for mb in range(M // P)])
-        ka_mx = [quantize_keys(ka_grouped[0], "ka0", "x_grouped1_0")]
+        x_mx.append([quantize(x_last, "x1_0")])
+        x_mx[1].append(quantize(interleave(x_raw[1][:, :, P:M], "x_grouped1_1", on_vector), "x1_1"))
         qa_grouped = [queries(mb) for mb in range(M // P)]
         qa_mx = [quantize(qa_grouped[mb], "qa%d" % mb) for mb in range(M // P)]
-        ka_mx.append(quantize_keys(ka_grouped[1], "ka1", "x1_codes0"))
+        ka_mx = [quantize_keys(ka_grouped[0], "ka0", "x_grouped1_0")]
+        ka_mx.append(quantize_keys(ka_grouped[1], "ka1", "x_grouped1_1"))
         for mb in range(M // P):
             scores(qa_mx[mb], mb)

@@ -38,6 +38,7 @@ def tile_list_kvt_act_kernel(
         keep = ctx.enter_context(tc.tile_pool(name="keep", bufs=1))
         shared = ctx.enter_context(tc.tile_pool(name="shared", bufs=1))
         placed = ctx.enter_context(tc.tile_pool(name="placed", bufs=1))
+        head = ctx.enter_context(tc.tile_pool(name="head", bufs=1))
         psum = ctx.enter_context(tc.psum_pool(name="psum", bufs=8))
 
         def held(shape, dtype, name):
@@ -68,7 +69,7 @@ def tile_list_kvt_act_kernel(
             nc.sync.dma_start(scale_win[e:P:SHIFT, :], scale_rows[e])
 
         nc.sync.dma_start(word_win[:, LEAD:T], table[:, LEAD:T])
-        wk_raw = shared.tile([P, PASSES, R], I32, name="wk_raw", tag="wk_raw", align_bytes=64)
+        wk_raw = head.tile([P, PASSES, R], I32, name="wk_raw", align_bytes=64, offset=0)
         nc.sync.dma_start(wk_raw[:], wk_words.rearrange("a p r i -> p a (r i)").bitcast(I32))
 
         def load_pass(src, a, name, offset=None):
@@ -100,7 +101,7 @@ def tile_list_kvt_act_kernel(
             )
 
         def deal_wk_scales():
-            wk_plane = shared.tile([P, PASSES, R // 4], I32, name="wk_plane", tag="picked0", align_bytes=64)
+            wk_plane = head.tile([P, PASSES, R // 4], I32, name="wk_plane", align_bytes=64, offset=0)
             nc.vector.tensor_copy(
                 wk_plane[:].rearrange("p a (t g) -> p a t g", t=4),
                 wk_scale_raw[:].rearrange("p a (g t) -> p a t g", t=4),
@@ -118,9 +119,9 @@ def tile_list_kvt_act_kernel(
             return codes, plane
 
         def quantize_keys(grouped, name, tag):
-            codes = shared.tile([P, BANK], U32, name=name + "_codes", tag=tag, align_bytes=64)
-            plane = held([P, BANK], U8, name + "_plane")
-            for b in range(BANK // P):
+            codes = shared.tile([P, HALF], U32, name=name + "_codes", tag=tag, align_bytes=64)
+            plane = held([P, HALF], U8, name + "_plane")
+            for b in range(HALF // P):
                 cols = slice(b * P, (b + 1) * P)
                 nc.vector.quantize_mx(out=codes[:, cols].bitcast(FP8X4), scales=plane[:, cols], in_=grouped[b][:])
             return codes, plane
@@ -140,18 +141,19 @@ def tile_list_kvt_act_kernel(
             engine_copy(dealt, source[:, 2 * u : 2 * u + 2])
             return grouped
 
-        def gather_words(h, tag):
-            picked = shared.tile([P, BANK], U32, name="picked%d" % h, tag=tag, align_bytes=64)
+        def gather_words(h, offset=None):
+            pool = shared if offset is None else head
+            picked = pool.tile([P, BANK], U32, name="picked%d" % h, align_bytes=64, offset=offset)
             cols = slice(h * BANK // 16, (h + 1) * BANK // 16)
             nc.vector.tensor_copy(picked[:], word_win[:].bitcast(U32).indirect(offsets[:, cols]))
             return picked
 
-        def part_words(picked, h, tag):
-            codes = shared.tile([P, PASSES, 2 * BANK], U8, name="tab_codes%d" % h, tag=tag, align_bytes=64)
-            nc.vector.tensor_copy(
-                codes[:].bitcast(U16),
-                picked[:].bitcast(U16).rearrange("p (j d) -> p d j", d=PASSES),
-            )
+        def part_words(picked, h, cuts, offset=None):
+            pool = shared if offset is None else head
+            codes = pool.tile([P, PASSES, BANK], U16, name="tab_codes%d" % h, align_bytes=64, offset=offset)
+            words = picked[:].bitcast(U16).rearrange("p (j d) -> p d j", d=PASSES)
+            for first, last in zip(cuts, cuts[1:]):
+                nc.vector.tensor_copy(codes[:, :, first:last], words[:, :, first:last])
             return codes
 
         def keys(codes, h):
@@ -166,7 +168,7 @@ def tile_list_kvt_act_kernel(
                             out=bank[:, t, :],
                             lhsT=wk_codes[:, a, t * P : (t + 1) * P].bitcast(FP8X4),
                             lhsT_scale=wk_plane[:, a, :].bitcast(U8)[:, t * P : (t + 1) * P],
-                            rhs=codes[:, a, 2 * b * P : 2 * (b + 1) * P].bitcast(FP4X4),
+                            rhs=codes[:, a, b * P : (b + 1) * P].bitcast(FP4X4),
                             rhs_scale=tab_planes[h][a][:, b * P : (b + 1) * P],
                             start=(a == 0 and t == 0),
                             stop=(a == PASSES - 1 and t == PACK - 1),
@@ -226,8 +228,8 @@ def tile_list_kvt_act_kernel(
                         out=bank[:],
                         lhsT=qa[0][:].bitcast(FP8X4),
                         lhsT_scale=qa[1][:],
-                        rhs=ka_mx[h][0][:, u * HALF : (u + 1) * HALF].bitcast(FP8X4),
-                        rhs_scale=ka_mx[h][1][:, u * HALF : (u + 1) * HALF],
+                        rhs=ka_mx[2 * h + u][0][:].bitcast(FP8X4),
+                        rhs_scale=ka_mx[2 * h + u][1][:],
                         start=True,
                         stop=True,
                     )
@@ -254,11 +256,12 @@ def tile_list_kvt_act_kernel(
             codes, plane = quantize(grouped, "x%d" % a, tag)
             return [(codes[:, mb * P : (mb + 1) * P], plane[:, mb * P : (mb + 1) * P]) for mb in range(M // P)]
 
-        tab_codes = [part_words(gather_words(0, "picked0"), 0, "tab_codes0")]
+        picked_first = gather_words(0)
         deal_wk_words()
         wk_plane = deal_wk_scales()
+        tab_codes = [part_words(picked_first, 0, [0, P, BANK], PASSES * R)]
         x_first = interleave(x_raw[0][:], "x_grouped0", on_scalar)
-        tab_codes.append(part_words(gather_words(1, "wk_raw"), 1, "tab_codes1"))
+        tab_codes.append(part_words(gather_words(1, PASSES * (R + 2 * BANK)), 1, [0, BANK]))
         wv_grouped = {(0, 0): group_wv(0, 0, on_vector), (0, 1): group_wv(0, 1, on_scalar)}
         ka_grouped = [keys(tab_codes[h], h) for h in range(HALVES)]
         x_mx = [quantize_x(x_first, 0)]
@@ -267,9 +270,11 @@ def tile_list_kvt_act_kernel(
             wv_grouped[1, u] = group_wv(1, u, on_vector)
         for u in range(2):
             wv_mx[1, u] = quantize(wv_grouped[1, u], "wv1_%d" % u)
+        ka_mx = [quantize_keys(ka_grouped[0][0:2], "ka0", "wv_grouped1_0")]
         for nb in range(N // P):
             values(nb, "vv_staged%d" % nb)
         wq_mx = [quantize_wq(group_wq(0), 0)]
+        ka_mx.append(quantize_keys(ka_grouped[0][2:4], "ka1", "wq_grouped0_0"))
         wq_last = group_wq(1)
         x_last = interleave(x_raw[1][:, :, 0:P], "x_grouped1_0", on_vector)
         wq_mx.append(quantize_wq(wq_last, 1))
@@ -277,7 +282,7 @@ def tile_list_kvt_act_kernel(
         x_mx[1].append(quantize(interleave(x_raw[1][:, :, P:M], "x_grouped1_1", on_vector), "x1_1"))
         qa_grouped = [queries(mb) for mb in range(M // P)]
         qa_mx = [quantize(qa_grouped[mb], "qa%d" % mb) for mb in range(M // P)]
-        ka_mx = [quantize_keys(ka_grouped[0], "ka0", "x_grouped1_0")]
-        ka_mx.append(quantize_keys(ka_grouped[1], "ka1", "x_grouped1_1"))
+        ka_mx.append(quantize_keys(ka_grouped[1][0:2], "ka2", "x_grouped1_0"))
+        ka_mx.append(quantize_keys(ka_grouped[1][2:4], "ka3", "x_grouped1_1"))
         for mb in range(M // P):
             scores(qa_mx[mb], mb)

@@ -234,7 +234,7 @@ def tile_list_kvt_act_kernel(
                         stop=True,
                     )
                     part = staged[:, h * BANK + u * HALF : h * BANK + (u + 1) * HALF]
-                    if h == 0:
+                    if u == 0 or (mb, h) == (0, 0):
                         nc.scalar.activation(part, bank[:], COPY, scale=SCORE_SCALE)
                     else:
                         nc.vector.tensor_scalar(part, bank[:], SCORE_SCALE, None, MULT)

@@ -24,7 +24,8 @@ K_PASS = P * PACK
 PASSES = K // K_PASS
 BANK = 512
 HALVES = J // BANK
-SHIFT = 16
+SPREAD = 4
+QUADS = 4
 HALF = 256
 LEAD = 1024
 SCORE_SCALE = 0.03125
@@ -47,26 +48,23 @@ def tile_list_kvt_act_kernel(
         offsets = keep.tile([P, J // 16], U16, name="offsets")
         nc.sync.dma_start(offsets[:], offs)
 
+        wk_scale_raw = held([P, PASSES, R // 4], I32, "wk_scale_raw")
+        nc.vector.memset(wk_scale_raw[:], 0)
         scale_win = shared.tile([P, T // 4], I32, name="scale_win", tag="scale_win", align_bytes=64)
         nc.vector.memset(scale_win[:], 0)
-        wk_scale_raw = held([P, PASSES, R // 4], I32, "wk_scale_raw")
-        nc.gpsimd.memset(wk_scale_raw[:], 0)
-        for q in range(4):
-            nc.gpsimd.dma_start(
-                wk_scale_raw[32 * q : 32 * q + 4, :, :],
-                wk_scales[:, 4 * q : 4 * q + 4, :].rearrange("a r c -> r a c").bitcast(I32),
-            )
-        moved_planes = [held([P, BANK // 4], I32, "moved_plane%d" % h) for h in range(HALVES)]
-        for moved in moved_planes:
-            nc.vector.memset(moved[:], 0)
+        tab_plane = held([P, PASSES, J // 4], I32, "tab_plane")
+        nc.vector.memset(tab_plane[:], 0)
 
         word_win = held([P, T], I32, "word_win")
         table = tab_words[0].rearrange("p t b -> p (t b)").bitcast(I32)
         nc.sync.dma_start(word_win[:, 0:LEAD], table[:, 0:LEAD])
+        for q in range(4):
+            nc.sync.dma_start(
+                wk_scale_raw[32 * q : 32 * q + 4, :, :],
+                wk_scales[:, 4 * q : 4 * q + 4, :].rearrange("a r c -> r a c").bitcast(I32),
+            )
 
-        scale_rows = tab_scales.rearrange("a (q e) t -> e q a t", e=4).bitcast(I32)
-        for e in range(4):
-            nc.sync.dma_start(scale_win[e:P:SHIFT, :], scale_rows[e])
+        nc.sync.dma_start(scale_win[0:P:SPREAD, :], tab_scales.rearrange("a q t -> q a t").bitcast(I32))
 
         nc.sync.dma_start(word_win[:, LEAD:T], table[:, LEAD:T])
         wk_raw = head.tile([P, PASSES, R], I32, name="wk_raw", align_bytes=64, offset=0)
@@ -79,18 +77,22 @@ def tile_list_kvt_act_kernel(
             nc.sync.dma_start(raw[:], rows.rearrange("(p s) w -> p s w", s=PACK))
             return raw
 
-        x_raw = [load_pass(x, 0, "x_raw0")]
+        x_raw = [load_pass(x, 0, "x_raw0", 18 * BANK)]
+
+        picked_plane = held([P, J], U8, "picked_plane")
+        nc.vector.tensor_copy(picked_plane[:], scale_win[:].bitcast(U8).indirect(offsets[:]))
+        for q in range(QUADS):
+            nc.sync.dma_start(
+                tab_plane[32 * q : 32 * q + 4, :, :].rearrange("p a j -> p (a j)"),
+                picked_plane[32 * q : 32 * q + 32 : SPREAD, :].bitcast(I32),
+            )
+        tab_planes = [
+            [tab_plane[:, a, :].bitcast(U8)[:, h * BANK : (h + 1) * BANK] for a in range(PASSES)] for h in range(HALVES)
+        ]
+
         wv_raw = [load_pass(wv, 0, "wv_raw0", 2 * BANK), load_pass(wv, 1, "wv_raw1")]
         wq_raw = [load_pass(wq, a, "wq_raw%d" % a) for a in range(PASSES)]
         x_raw.append(load_pass(x, 1, "x_raw1"))
-
-        tab_planes = []
-        for h in range(HALVES):
-            picked_plane = held([P, BANK], U8, "picked_plane%d" % h)
-            cols = slice(h * BANK // 16, (h + 1) * BANK // 16)
-            nc.vector.tensor_copy(picked_plane[:], scale_win[:].bitcast(U8).indirect(offsets[:, cols]))
-            nc.scalar.dma_start(moved_planes[h][0 : P - SHIFT, :], picked_plane[SHIFT:P, :].bitcast(I32))
-            tab_planes.append([picked_plane[:], moved_planes[h][:].bitcast(U8)])
 
         wk_codes = held([P, PASSES, R], I32, "wk_codes")
 
@@ -101,7 +103,7 @@ def tile_list_kvt_act_kernel(
             )
 
         def deal_wk_scales():
-            wk_plane = head.tile([P, PASSES, R // 4], I32, name="wk_plane", align_bytes=64, offset=0)
+            wk_plane = held([P, PASSES, R // 4], I32, "wk_plane")
             nc.vector.tensor_copy(
                 wk_plane[:].rearrange("p a (t g) -> p a t g", t=4),
                 wk_scale_raw[:].rearrange("p a (g t) -> p a t g", t=4),
@@ -160,7 +162,7 @@ def tile_list_kvt_act_kernel(
             grouped = []
             for b in range(BANK // P):
                 n = h * BANK // P + b
-                grouped.append(placed.tile([P, BANK], BF16, name="ka_grouped%d" % n, align_bytes=64, offset=n * 2 * BANK))
+                grouped.append(placed.tile([P, BANK], BF16, name="ka_grouped%d" % n, align_bytes=64, offset=(n or 9) * 2 * BANK))
                 bank = psum.tile([P, PACK, P], F32, name="k_bank", tag="bank")
                 for a in range(PASSES):
                     for t in range(PACK):

@@ -48,23 +48,19 @@ def tile_list_kvt_act_kernel(
         offsets = keep.tile([P, J // 16], U16, name="offsets")
         nc.sync.dma_start(offsets[:], offs)
 
-        wk_scale_raw = held([P, PASSES, R // 4], I32, "wk_scale_raw")
-        nc.vector.memset(wk_scale_raw[:], 0)
-        scale_win = shared.tile([P, T // 4], I32, name="scale_win", tag="scale_win", align_bytes=64)
+        scale_win = held([P, T // 4], I32, "scale_win")
         nc.vector.memset(scale_win[:], 0)
-        tab_plane = held([P, PASSES, J // 4], I32, "tab_plane")
-        nc.vector.memset(tab_plane[:], 0)
+        wk_scale_raw = held([P, R // 4], I32, "wk_scale_raw")
+        nc.vector.memset(wk_scale_raw[:], 0)
+        planes = held([P, PASSES, (J + R) // 4], I32, "planes")
+        nc.vector.memset(planes[:], 0)
 
         word_win = held([P, T], I32, "word_win")
         table = tab_words[0].rearrange("p t b -> p (t b)").bitcast(I32)
         nc.sync.dma_start(word_win[:, 0:LEAD], table[:, 0:LEAD])
-        for q in range(4):
-            nc.sync.dma_start(
-                wk_scale_raw[32 * q : 32 * q + 4, :, :],
-                wk_scales[:, 4 * q : 4 * q + 4, :].rearrange("a r c -> r a c").bitcast(I32),
-            )
 
         nc.sync.dma_start(scale_win[0:P:SPREAD, :], tab_scales.rearrange("a q t -> q a t").bitcast(I32))
+        nc.sync.dma_start(wk_scale_raw[0:P:SPREAD, :], wk_scales.rearrange("a q r -> q a r").bitcast(I32))
 
         nc.sync.dma_start(word_win[:, LEAD:T], table[:, LEAD:T])
         wk_raw = head.tile([P, PASSES, R], I32, name="wk_raw", align_bytes=64, offset=0)
@@ -79,36 +75,35 @@ def tile_list_kvt_act_kernel(
 
         x_raw = [load_pass(x, 0, "x_raw0", 18 * BANK)]
 
+        spread_rows = held([P, (J + R) // 4], I32, "spread_rows")
+        nc.vector.tensor_copy(
+            spread_rows[:, J // 4 :].rearrange("p (t g) -> p t g", t=4),
+            wk_scale_raw[:].rearrange("p (g t) -> p t g", t=4),
+        )
         picked_plane = held([P, J], U8, "picked_plane")
         nc.vector.tensor_copy(picked_plane[:], scale_win[:].bitcast(U8).indirect(offsets[:]))
+        nc.vector.tensor_copy(spread_rows[:, 0 : J // 4], picked_plane[:].bitcast(I32))
         for q in range(QUADS):
             nc.sync.dma_start(
-                tab_plane[32 * q : 32 * q + 4, :, :].rearrange("p a j -> p (a j)"),
-                picked_plane[32 * q : 32 * q + 32 : SPREAD, :].bitcast(I32),
+                planes[32 * q : 32 * q + 4, :, :].rearrange("p a j -> p (a j)"),
+                spread_rows[32 * q : 32 * q + 32 : SPREAD, :],
             )
         tab_planes = [
-            [tab_plane[:, a, :].bitcast(U8)[:, h * BANK : (h + 1) * BANK] for a in range(PASSES)] for h in range(HALVES)
+            [planes[:, a, :].bitcast(U8)[:, h * BANK : (h + 1) * BANK] for a in range(PASSES)] for h in range(HALVES)
         ]
+        wk_planes = [planes[:, a, :].bitcast(U8)[:, J : J + R] for a in range(PASSES)]
 
-        wv_raw = [load_pass(wv, 0, "wv_raw0", 2 * BANK), load_pass(wv, 1, "wv_raw1")]
-        wq_raw = [load_pass(wq, a, "wq_raw%d" % a) for a in range(PASSES)]
+        wv_raw = [load_pass(wv, 0, "wv_raw0"), load_pass(wv, 1, "wv_raw1")]
+        wq_raw = [load_pass(wq, 0, "wq_raw0"), load_pass(wq, 1, "wq_raw1", 26 * BANK)]
         x_raw.append(load_pass(x, 1, "x_raw1"))
 
         wk_codes = held([P, PASSES, R], I32, "wk_codes")
 
         def deal_wk_words():
-            nc.vector.tensor_copy(
-                wk_codes[:].rearrange("p a (t g i) -> p a t g i", t=4, i=4),
-                wk_raw[:].rearrange("p a (g t i) -> p a t g i", t=4, i=4),
+            nc.scalar.copy(
+                wk_codes[:].bitcast(U32).rearrange("p a (t g i) -> p a t g i", t=4, i=4),
+                wk_raw[:].bitcast(U32).rearrange("p a (g t i) -> p a t g i", t=4, i=4),
             )
-
-        def deal_wk_scales():
-            wk_plane = held([P, PASSES, R // 4], I32, "wk_plane")
-            nc.vector.tensor_copy(
-                wk_plane[:].rearrange("p a (t g) -> p a t g", t=4),
-                wk_scale_raw[:].rearrange("p a (g t) -> p a t g", t=4),
-            )
-            return wk_plane
 
         def quantize(grouped, name, tag=None):
             width = grouped.shape[1] // PACK
@@ -143,20 +138,17 @@ def tile_list_kvt_act_kernel(
             engine_copy(dealt, source[:, 2 * u : 2 * u + 2])
             return grouped
 
-        def gather_words(h, offset=None):
-            pool = shared if offset is None else head
-            picked = pool.tile([P, BANK], U32, name="picked%d" % h, align_bytes=64, offset=offset)
-            cols = slice(h * BANK // 16, (h + 1) * BANK // 16)
-            nc.vector.tensor_copy(picked[:], word_win[:].bitcast(U32).indirect(offsets[:, cols]))
-            return picked
+        picked = held([P, BANK + HALF], U32, "picked")
+        tab_codes = [held([P, PASSES, BANK], U16, "tab_codes%d" % h) for h in range(HALVES)]
 
-        def part_words(picked, h, cuts, offset=None):
-            pool = shared if offset is None else head
-            codes = pool.tile([P, PASSES, BANK], U16, name="tab_codes%d" % h, align_bytes=64, offset=offset)
-            words = picked[:].bitcast(U16).rearrange("p (j d) -> p d j", d=PASSES)
-            for first, last in zip(cuts, cuts[1:]):
-                nc.vector.tensor_copy(codes[:, :, first:last], words[:, :, first:last])
-            return codes
+        def gather_words(first, last, place):
+            listed = offsets[:, first // 16 : last // 16]
+            nc.vector.tensor_copy(picked[:, place : place + last - first], word_win[:].bitcast(U32).indirect(listed))
+
+        def part_words(first, last, place):
+            h = first // BANK
+            words = picked[:, place : place + last - first].bitcast(U16).rearrange("p (j d) -> p d j", d=PASSES)
+            nc.vector.tensor_copy(tab_codes[h][:, :, first - h * BANK : last - h * BANK], words)
 
         def keys(codes, h):
             grouped = []
@@ -169,7 +161,7 @@ def tile_list_kvt_act_kernel(
                         nc.tensor.matmul_mx(
                             out=bank[:, t, :],
                             lhsT=wk_codes[:, a, t * P : (t + 1) * P].bitcast(FP8X4),
-                            lhsT_scale=wk_plane[:, a, :].bitcast(U8)[:, t * P : (t + 1) * P],
+                            lhsT_scale=wk_planes[a][:, t * P : (t + 1) * P],
                             rhs=codes[:, a, b * P : (b + 1) * P].bitcast(FP4X4),
                             rhs_scale=tab_planes[h][a][:, b * P : (b + 1) * P],
                             start=(a == 0 and t == 0),
@@ -182,8 +174,11 @@ def tile_list_kvt_act_kernel(
                 )
             return grouped
 
-        def values(nb, tag):
-            staged = shared.tile([P, J], F32, name="vv_staged%d" % nb, tag=tag, align_bytes=64)
+        def values(nb):
+            if nb < 2:
+                staged = held([P, J], F32, "vv_staged%d" % nb)
+            else:
+                staged = placed.tile([P, J], F32, name="vv_staged%d" % nb, align_bytes=64, offset=(10 + 8 * nb) * BANK)
             for h in range(HALVES):
                 bank = psum.tile([P, BANK], F32, name="v_bank", tag="bank")
                 for a in reversed(range(PASSES)):
@@ -248,8 +243,9 @@ def tile_list_kvt_act_kernel(
         def group_wv(a, u, engine_copy):
             return interleave(wv_raw[a][:, :, u * HALF : (u + 1) * HALF], "wv_grouped%d_%d" % (a, u), engine_copy)
 
-        def group_wq(a):
-            return [interleave_wq(wq_raw[a][:], u, "wq_grouped%d_%d" % (a, u), on_vector) for u in range(2)]
+        def group_wq(a, second):
+            engines = [on_vector, second]
+            return [interleave_wq(wq_raw[a][:], u, "wq_grouped%d_%d" % (a, u), engines[u]) for u in range(2)]
 
         def quantize_wq(grouped, a):
             return [quantize(grouped[u], "wq%d_%d" % (a, u)) for u in range(2)]
@@ -258,13 +254,26 @@ def tile_list_kvt_act_kernel(
             codes, plane = quantize(grouped, "x%d" % a, tag)
             return [(codes[:, mb * P : (mb + 1) * P], plane[:, mb * P : (mb + 1) * P]) for mb in range(M // P)]
 
-        picked_first = gather_words(0)
+        warm = psum.tile([P, BANK], F32, name="warm_bank", tag="bank")
+        for n in range(4):
+            nc.tensor.matmul_mx(
+                out=warm[:],
+                lhsT=wk_raw[:, 0, 0:P].bitcast(FP8X4),
+                lhsT_scale=wk_scale_raw[:].bitcast(U8)[:, 0:P],
+                rhs=wk_raw[:, 0, :].bitcast(FP8X4),
+                rhs_scale=wk_scale_raw[:].bitcast(U8),
+                start=True,
+                stop=True,
+            )
+        gather_words(0, HALF, 0)
+        gather_words(HALF, BANK, BANK)
+        part_words(0, HALF, 0)
+        gather_words(BANK, J, 0)
+        part_words(HALF, BANK, BANK)
+        part_words(BANK, J, 0)
         deal_wk_words()
-        wk_plane = deal_wk_scales()
-        tab_codes = [part_words(picked_first, 0, [0, P, BANK], PASSES * R)]
         x_first = interleave(x_raw[0][:], "x_grouped0", on_scalar)
-        tab_codes.append(part_words(gather_words(1, PASSES * (R + 2 * BANK)), 1, [0, BANK]))
-        wv_grouped = {(0, 0): group_wv(0, 0, on_vector), (0, 1): group_wv(0, 1, on_scalar)}
+        wv_grouped = {(0, u): group_wv(0, u, on_vector) for u in range(2)}
         ka_grouped = [keys(tab_codes[h], h) for h in range(HALVES)]
         x_mx = [quantize_x(x_first, 0)]
         wv_mx = {(0, u): quantize(wv_grouped[0, u], "wv0_%d" % u) for u in range(2)}
@@ -273,11 +282,13 @@ def tile_list_kvt_act_kernel(
         for u in range(2):
             wv_mx[1, u] = quantize(wv_grouped[1, u], "wv1_%d" % u)
         ka_mx = [quantize_keys(ka_grouped[0][0:2], "ka0", "wv_grouped1_0")]
-        for nb in range(N // P):
-            values(nb, "vv_staged%d" % nb)
-        wq_mx = [quantize_wq(group_wq(0), 0)]
+        for nb in range(2):
+            values(nb)
+        wq_mx = [quantize_wq(group_wq(0, on_vector), 0)]
         ka_mx.append(quantize_keys(ka_grouped[0][2:4], "ka1", "wq_grouped0_0"))
-        wq_last = group_wq(1)
+        wq_last = group_wq(1, on_scalar)
+        for nb in range(2, N // P):
+            values(nb)
         x_last = interleave(x_raw[1][:, :, 0:P], "x_grouped1_0", on_vector)
         wq_mx.append(quantize_wq(wq_last, 1))
         x_mx.append([quantize(x_last, "x1_0")])

@@ -184,8 +184,8 @@ def tile_list_kvt_act_kernel(
                 for a in reversed(range(PASSES)):
                     nc.tensor.matmul_mx(
                         out=bank[:],
-                        lhsT=wv_mx[a, nb // 2][0][:, nb % 2 * P : (nb % 2 + 1) * P].bitcast(FP8X4),
-                        lhsT_scale=wv_mx[a, nb // 2][1][:, nb % 2 * P : (nb % 2 + 1) * P],
+                        lhsT=wv_mx[a][nb][0].bitcast(FP8X4),
+                        lhsT_scale=wv_mx[a][nb][1],
                         rhs=tab_codes[h][:, a, :].bitcast(FP4X4),
                         rhs_scale=tab_planes[h][a],
                         start=(a == PASSES - 1),
@@ -207,7 +207,8 @@ def tile_list_kvt_act_kernel(
                         start=(a == 0 and t == 0),
                         stop=(a == PASSES - 1 and t == PACK - 1),
                     )
-            grouped = held([P, PACK * P], BF16, "qa_grouped%d" % mb)
+            name = "qa_grouped%d" % mb
+            grouped = shared.tile([P, PACK * P], BF16, name=name, tag=name, align_bytes=64)
             out = grouped[:].rearrange("p (m t) -> p m t", t=PACK)
             sums = bank[:].rearrange("p t m -> p m t")
             if mb == 0:
@@ -240,8 +241,12 @@ def tile_list_kvt_act_kernel(
 
         on_vector, on_scalar = nc.vector.tensor_copy, nc.scalar.copy
 
-        def group_wv(a, u, engine_copy):
-            return interleave(wv_raw[a][:, :, u * HALF : (u + 1) * HALF], "wv_grouped%d_%d" % (a, u), engine_copy)
+        def group_wv(a, first, last):
+            return interleave(wv_raw[a][:, :, first:last], "wv_grouped%d_%d" % (a, first // P), on_vector)
+
+        def quantize_wv(grouped, name):
+            codes, plane = quantize(grouped, name)
+            return [(codes[:, c : c + P], plane[:, c : c + P]) for c in range(0, codes.shape[1], P)]
 
         def group_wq(a, second):
             engines = [on_vector, second]
@@ -273,29 +278,30 @@ def tile_list_kvt_act_kernel(
         part_words(BANK, J, 0)
         deal_wk_words()
         x_first = interleave(x_raw[0][:], "x_grouped0", on_scalar)
-        wv_grouped = {(0, u): group_wv(0, u, on_vector) for u in range(2)}
+        wv_first = [group_wv(0, 0, HALF), group_wv(0, HALF, N)]
         ka_grouped = [keys(tab_codes[h], h) for h in range(HALVES)]
         x_mx = [quantize_x(x_first, 0)]
-        wv_mx = {(0, u): quantize(wv_grouped[0, u], "wv0_%d" % u) for u in range(2)}
-        for u in range(2):
-            wv_grouped[1, u] = group_wv(1, u, on_vector)
-        for u in range(2):
-            wv_mx[1, u] = quantize(wv_grouped[1, u], "wv1_%d" % u)
-        ka_mx = [quantize_keys(ka_grouped[0][0:2], "ka0", "wv_grouped1_0")]
+        wv_mx = [quantize_wv(wv_first[0], "wv0_0") + quantize_wv(wv_first[1], "wv0_2")]
+        wv_last = [group_wv(1, 0, P), group_wv(1, P, HALF)]
+        wv_mx.append(quantize_wv(wv_last[0], "wv1_0"))
+        wv_last.append(group_wv(1, HALF, N))
+        wv_mx[1].extend(quantize_wv(wv_last[1], "wv1_1") + quantize_wv(wv_last[2], "wv1_2"))
+        ka_mx = [quantize_keys(ka_grouped[0][0:2], "ka0", "wv_grouped1_1")]
         for nb in range(2):
             values(nb)
         wq_mx = [quantize_wq(group_wq(0, on_vector), 0)]
-        ka_mx.append(quantize_keys(ka_grouped[0][2:4], "ka1", "wq_grouped0_0"))
         wq_last = group_wq(1, on_scalar)
         for nb in range(2, N // P):
             values(nb)
         x_last = interleave(x_raw[1][:, :, 0:P], "x_grouped1_0", on_vector)
         wq_mx.append(quantize_wq(wq_last, 1))
         x_mx.append([quantize(x_last, "x1_0")])
-        x_mx[1].append(quantize(interleave(x_raw[1][:, :, P:M], "x_grouped1_1", on_vector), "x1_1"))
+        x_rest = interleave(x_raw[1][:, :, P:M], "x_grouped1_1", on_vector)
+        ka_mx.append(quantize_keys(ka_grouped[0][2:4], "ka1", "x_grouped1_0"))
+        x_mx[1].append(quantize(x_rest, "x1_1"))
         qa_grouped = [queries(mb) for mb in range(M // P)]
         qa_mx = [quantize(qa_grouped[mb], "qa%d" % mb) for mb in range(M // P)]
-        ka_mx.append(quantize_keys(ka_grouped[1][0:2], "ka2", "x_grouped1_0"))
+        ka_mx.append(quantize_keys(ka_grouped[1][0:2], "ka2", "qa_grouped0"))
         ka_mx.append(quantize_keys(ka_grouped[1][2:4], "ka3", "x_grouped1_1"))
         for mb in range(M // P):
             scores(qa_mx[mb], mb)

@@ -259,17 +259,6 @@ def tile_list_kvt_act_kernel(
             codes, plane = quantize(grouped, "x%d" % a, tag)
             return [(codes[:, mb * P : (mb + 1) * P], plane[:, mb * P : (mb + 1) * P]) for mb in range(M // P)]
 
-        warm = psum.tile([P, BANK], F32, name="warm_bank", tag="bank")
-        for n in range(4):
-            nc.tensor.matmul_mx(
-                out=warm[:],
-                lhsT=wk_raw[:, 0, 0:P].bitcast(FP8X4),
-                lhsT_scale=wk_scale_raw[:].bitcast(U8)[:, 0:P],
-                rhs=wk_raw[:, 0, :].bitcast(FP8X4),
-                rhs_scale=wk_scale_raw[:].bitcast(U8),
-                start=True,
-                stop=True,
-            )
         gather_words(0, HALF, 0)
         gather_words(HALF, BANK, BANK)
         part_words(0, HALF, 0)

@@ -51,9 +51,12 @@ def tile_list_kvt_act_kernel(
         scale_win = held([P, T // 4], I32, "scale_win")
         nc.vector.memset(scale_win[:], 0)
         wk_scale_raw = held([P, R // 4], I32, "wk_scale_raw")
-        nc.vector.memset(wk_scale_raw[:], 0)
+        nc.vector.memset(wk_scale_raw[:, 0 : R // 8], 0)
+        nc.vector.memset(wk_scale_raw[:, R // 8 :], 0)
         planes = held([P, PASSES, (J + R) // 4], I32, "planes")
-        nc.vector.memset(planes[:], 0)
+        for a in range(PASSES):
+            nc.vector.memset(planes[:, a, 0 : J // 4], 0)
+            nc.vector.memset(planes[:, a, J // 4 :], 0)
 
         word_win = held([P, T], I32, "word_win")
         table = tab_words[0].rearrange("p t b -> p (t b)").bitcast(I32)
@@ -81,8 +84,12 @@ def tile_list_kvt_act_kernel(
             wk_scale_raw[:].rearrange("p (g t) -> p t g", t=4),
         )
         picked_plane = held([P, J], U8, "picked_plane")
-        nc.vector.tensor_copy(picked_plane[:], scale_win[:].bitcast(U8).indirect(offsets[:]))
-        nc.vector.tensor_copy(spread_rows[:, 0 : J // 4], picked_plane[:].bitcast(I32))
+        for h in range(HALVES):
+            listed = offsets[:, h * BANK // 16 : (h + 1) * BANK // 16]
+            nc.vector.tensor_copy(picked_plane[:, h * BANK : (h + 1) * BANK], scale_win[:].bitcast(U8).indirect(listed))
+        for h in range(HALVES):
+            words = slice(h * BANK // 4, (h + 1) * BANK // 4)
+            nc.vector.tensor_copy(spread_rows[:, words], picked_plane[:].bitcast(I32)[:, words])
         for q in range(QUADS):
             nc.sync.dma_start(
                 planes[32 * q : 32 * q + 4, :, :].rearrange("p a j -> p (a j)"),
@@ -263,8 +270,10 @@ def tile_list_kvt_act_kernel(
         gather_words(HALF, BANK, BANK)
         part_words(0, HALF, 0)
         gather_words(BANK, J, 0)
-        part_words(HALF, BANK, BANK)
-        part_words(BANK, J, 0)
+        part_words(HALF, HALF + P, BANK)
+        part_words(HALF + P, BANK, BANK + P)
+        part_words(BANK, BANK + HALF, 0)
+        part_words(BANK + HALF, J, HALF)
         deal_wk_words()
         x_first = interleave(x_raw[0][:], "x_grouped0", on_scalar)
         wv_first = [group_wv(0, 0, HALF), group_wv(0, HALF, N)]

from contextlib import ExitStack

import concourse.mybir as mybir

K, R, M, N, T, J = 1024, 512, 256, 512, 4096, 1024
FLOPS = 2 * K * R * M + 2 * K * R * J + 2 * R * M * J + 2 * K * N * J

F32 = mybir.dt.float32
BF16 = mybir.dt.bfloat16
I32 = mybir.dt.int32
U32 = mybir.dt.uint32
U16 = mybir.dt.uint16
U8 = mybir.dt.uint8
FP8X4 = mybir.dt.float8_e4m3fn_x4
FP4X4 = mybir.dt.float4_e2m1fn_x4
RELU = mybir.ActivationFunctionType.Relu
COPY = mybir.ActivationFunctionType.Copy
MAX = mybir.AluOpType.max
MULT = mybir.AluOpType.mult

P = 128
PACK = 4
K_PASS = P * PACK
PASSES = K // K_PASS
BANK = 512
HALVES = J // BANK
SPREAD = 4
QUADS = 4
HALF = 256
LEAD = 1024
SCORE_SCALE = 0.03125


def tile_list_kvt_act_kernel(
    tc, tab_words, tab_scales, x, wq, wk_words, wk_scales, wv, offs, out_0, out_1
):
    nc = tc.nc
    with ExitStack() as ctx:
        keep = ctx.enter_context(tc.tile_pool(name="keep", bufs=1))
        shared = ctx.enter_context(tc.tile_pool(name="shared", bufs=1))
        placed = ctx.enter_context(tc.tile_pool(name="placed", bufs=1))
        head = ctx.enter_context(tc.tile_pool(name="head", bufs=1))
        psum = ctx.enter_context(tc.psum_pool(name="psum", bufs=8))

        def held(shape, dtype, name):
            return keep.tile(shape, dtype, name=name, align_bytes=64)

        offsets = keep.tile([P, J // 16], U16, name="offsets")
        nc.sync.dma_start(offsets[:], offs)

        scale_win = held([P, T // 4], I32, "scale_win")
        nc.vector.memset(scale_win[:], 0)
        wk_scale_raw = held([P, R // 4], I32, "wk_scale_raw")
        nc.vector.memset(wk_scale_raw[:, 0 : R // 8], 0)
        nc.vector.memset(wk_scale_raw[:, R // 8 :], 0)
        planes = held([P, PASSES, (J + R) // 4], I32, "planes")
        for a in range(PASSES):
            nc.vector.memset(planes[:, a, 0 : J // 4], 0)
            nc.vector.memset(planes[:, a, J // 4 :], 0)

        word_win = held([P, T], I32, "word_win")
        table = tab_words[0].rearrange("p t b -> p (t b)").bitcast(I32)
        nc.sync.dma_start(word_win[:, 0:LEAD], table[:, 0:LEAD])

        nc.sync.dma_start(scale_win[0:P:SPREAD, :], tab_scales.rearrange("a q t -> q a t").bitcast(I32))
        nc.sync.dma_start(wk_scale_raw[0:P:SPREAD, :], wk_scales.rearrange("a q r -> q a r").bitcast(I32))

        nc.sync.dma_start(word_win[:, LEAD:T], table[:, LEAD:T])
        wk_raw = head.tile([P, PASSES, R], I32, name="wk_raw", align_bytes=64, offset=0)
        nc.sync.dma_start(wk_raw[:], wk_words.rearrange("a p r i -> p a (r i)").bitcast(I32))

        def load_pass(src, a, name, offset=None):
            pool = shared if offset is None else placed
            raw = pool.tile([P, PACK, src.shape[1]], F32, name=name + "_raw", tag=name, align_bytes=64, offset=offset)
            rows = src[a * K_PASS : (a + 1) * K_PASS, :]
            nc.sync.dma_start(raw[:], rows.rearrange("(p s) w -> p s w", s=PACK))
            return raw

        x_raw = [load_pass(x, 0, "x_raw0", 18 * BANK)]

        spread_rows = held([P, (J + R) // 4], I32, "spread_rows")
        nc.vector.tensor_copy(
            spread_rows[:, J // 4 :].rearrange("p (t g) -> p t g", t=4),
            wk_scale_raw[:].rearrange("p (g t) -> p t g", t=4),
        )
        picked_plane = held([P, J], U8, "picked_plane")
        for h in range(HALVES):
            listed = offsets[:, h * BANK // 16 : (h + 1) * BANK // 16]
            nc.vector.tensor_copy(picked_plane[:, h * BANK : (h + 1) * BANK], scale_win[:].bitcast(U8).indirect(listed))
        for h in range(HALVES):
            words = slice(h * BANK // 4, (h + 1) * BANK // 4)
            nc.vector.tensor_copy(spread_rows[:, words], picked_plane[:].bitcast(I32)[:, words])
        for q in range(QUADS):
            nc.sync.dma_start(
                planes[32 * q : 32 * q + 4, :, :].rearrange("p a j -> p (a j)"),
                spread_rows[32 * q : 32 * q + 32 : SPREAD, :],
            )
        tab_planes = [
            [planes[:, a, :].bitcast(U8)[:, h * BANK : (h + 1) * BANK] for a in range(PASSES)] for h in range(HALVES)
        ]
        wk_planes = [planes[:, a, :].bitcast(U8)[:, J : J + R] for a in range(PASSES)]

        wv_raw = [load_pass(wv, 0, "wv_raw0"), load_pass(wv, 1, "wv_raw1")]
        wq_raw = [load_pass(wq, 0, "wq_raw0"), load_pass(wq, 1, "wq_raw1", 26 * BANK)]
        x_raw.append(load_pass(x, 1, "x_raw1"))

        wk_codes = held([P, PASSES, R], I32, "wk_codes")

        def deal_wk_words():
            nc.scalar.copy(
                wk_codes[:].bitcast(U32).rearrange("p a (t g i) -> p a t g i", t=4, i=4),
                wk_raw[:].bitcast(U32).rearrange("p a (g t i) -> p a t g i", t=4, i=4),
            )

        def quantize(grouped, name, tag=None):
            width = grouped.shape[1] // PACK
            if tag is None:
                codes = held([P, width], U32, name + "_codes")
            else:
                codes = shared.tile([P, width], U32, name=name + "_codes", tag=tag, align_bytes=64)
            plane = held([P, width], U8, name + "_plane")
            nc.vector.quantize_mx(out=codes[:].bitcast(FP8X4), scales=plane[:], in_=grouped[:])
            return codes, plane

        def quantize_keys(grouped, name, tag):
            codes = shared.tile([P, HALF], U32, name=name + "_codes", tag=tag, align_bytes=64)
            plane = held([P, HALF], U8, name + "_plane")
            for b in range(HALF // P):
                cols = slice(b * P, (b + 1) * P)
                nc.vector.quantize_mx(out=codes[:, cols].bitcast(FP8X4), scales=plane[:, cols], in_=grouped[b][:])
            return codes, plane

        def interleave(raw, name, engine_copy):
            grouped = shared.tile([P, PACK * raw.shape[2]], BF16, name=name, tag=name, align_bytes=64)
            engine_copy(
                grouped[:].rearrange("p (c i s) -> p c s i", i=2, s=PACK),
                raw.rearrange("p s (c i) -> p c s i", i=2),
            )
            return grouped

        def interleave_wq(raw, u, name, engine_copy):
            grouped = shared.tile([P, PACK * HALF], BF16, name=name, tag=name, align_bytes=64)
            dealt = grouped[:].rearrange("p (t g i s) -> p t g s i", t=2, i=4, s=PACK)
            source = raw.rearrange("p s (g t i) -> p t g s i", t=4, i=4)
            engine_copy(dealt, source[:, 2 * u : 2 * u + 2])
            return grouped

        picked = held([P, BANK + HALF], U32, "picked")
        tab_codes = [held([P, PASSES, BANK], U16, "tab_codes%d" % h) for h in range(HALVES)]

        def gather_words(first, last, place):
            listed = offsets[:, first // 16 : last // 16]
            nc.vector.tensor_copy(picked[:, place : place + last - first], word_win[:].bitcast(U32).indirect(listed))

        def part_words(first, last, place):
            h = first // BANK
            words = picked[:, place : place + last - first].bitcast(U16).rearrange("p (j d) -> p d j", d=PASSES)
            nc.vector.tensor_copy(tab_codes[h][:, :, first - h * BANK : last - h * BANK], words)

        def keys(codes, h):
            grouped = []
            for b in range(BANK // P):
                n = h * BANK // P + b
                grouped.append(placed.tile([P, BANK], BF16, name="ka_grouped%d" % n, align_bytes=64, offset=(n or 9) * 2 * BANK))
                bank = psum.tile([P, PACK, P], F32, name="k_bank", tag="bank")
                for a in range(PASSES):
                    for t in range(PACK):
                        nc.tensor.matmul_mx(
                            out=bank[:, t, :],
                            lhsT=wk_codes[:, a, t * P : (t + 1) * P].bitcast(FP8X4),
                            lhsT_scale=wk_planes[a][:, t * P : (t + 1) * P],
                            rhs=codes[:, a, b * P : (b + 1) * P].bitcast(FP4X4),
                            rhs_scale=tab_planes[h][a][:, b * P : (b + 1) * P],
                            start=(a == 0 and t == 0),
                            stop=(a == PASSES - 1 and t == PACK - 1),
                        )
                nc.scalar.activation(
                    grouped[b][:].rearrange("p (j t) -> p j t", t=PACK),
                    bank[:].rearrange("p t j -> p j t"),
                    RELU,
                )
            return grouped

        def values(nb):
            if nb < 2:
                staged = held([P, J], F32, "vv_staged%d" % nb)
            else:
                staged = placed.tile([P, J], F32, name="vv_staged%d" % nb, align_bytes=64, offset=(10 + 8 * nb) * BANK)
            for h in range(HALVES):
                bank = psum.tile([P, BANK], F32, name="v_bank", tag="bank")
                for a in reversed(range(PASSES)):
                    nc.tensor.matmul_mx(
                        out=bank[:],
                        lhsT=wv_mx[a][nb][0].bitcast(FP8X4),
                        lhsT_scale=wv_mx[a][nb][1],
                        rhs=tab_codes[h][:, a, :].bitcast(FP4X4),
                        rhs_scale=tab_planes[h][a],
                        start=(a == PASSES - 1),
                        stop=(a == 0),
                    )
                nc.scalar.copy(staged[:, h * BANK : (h + 1) * BANK], bank[:])
            nc.sync.dma_start(out_1[nb * P : (nb + 1) * P, :], staged[:])

        def queries(mb):
            bank = psum.tile([P, PACK, P], F32, name="q_bank", tag="bank")
            for a in range(PASSES):
                for t in range(PACK):
                    nc.tensor.matmul_mx(
                        out=bank[:, t, :],
                        lhsT=wq_mx[a][t // 2][0][:, t % 2 * P : (t % 2 + 1) * P].bitcast(FP8X4),
                        lhsT_scale=wq_mx[a][t // 2][1][:, t % 2 * P : (t % 2 + 1) * P],
                        rhs=x_mx[a][mb][0][:].bitcast(FP8X4),
                        rhs_scale=x_mx[a][mb][1][:],
                        start=(a == 0 and t == 0),
                        stop=(a == PASSES - 1 and t == PACK - 1),
                    )
            name = "qa_grouped%d" % mb
            grouped = shared.tile([P, PACK * P], BF16, name=name, tag=name, align_bytes=64)
            out = grouped[:].rearrange("p (m t) -> p m t", t=PACK)
            sums = bank[:].rearrange("p t m -> p m t")
            if mb == 0:
                nc.vector.tensor_scalar(out, sums, 0.0, None, MAX)
            else:
                nc.scalar.activation(out, sums, RELU)
            return grouped

        def scores(qa, mb):
            staged = held([P, J], F32, "sc_staged%d" % mb)
            for h in range(HALVES):
                for u in range(2):
                    bank = psum.tile([P, HALF], F32, name="s_bank", tag="bank")
                    nc.tensor.matmul_mx(
                        out=bank[:],
                        lhsT=qa[0][:].bitcast(FP8X4),
                        lhsT_scale=qa[1][:],
                        rhs=ka_mx[2 * h + u][0][:].bitcast(FP8X4),
                        rhs_scale=ka_mx[2 * h + u][1][:],
                        start=True,
                        stop=True,
                    )
                    part = staged[:, h * BANK + u * HALF : h * BANK + (u + 1) * HALF]
                    if u == 0 or (mb, h) == (0, 0):
                        nc.scalar.activation(part, bank[:], COPY, scale=SCORE_SCALE)
                    else:
                        nc.vector.tensor_scalar(part, bank[:], SCORE_SCALE, None, MULT)
                cols = slice(h * BANK, (h + 1) * BANK)
                nc.sync.dma_start(out_0[mb * P : (mb + 1) * P, cols], staged[:, cols])

        on_vector, on_scalar = nc.vector.tensor_copy, nc.scalar.copy

        def group_wv(a, first, last):
            return interleave(wv_raw[a][:, :, first:last], "wv_grouped%d_%d" % (a, first // P), on_vector)

        def quantize_wv(grouped, name):
            codes, plane = quantize(grouped, name)
            return [(codes[:, c : c + P], plane[:, c : c + P]) for c in range(0, codes.shape[1], P)]

        def group_wq(a, second):
            engines = [on_vector, second]
            return [interleave_wq(wq_raw[a][:], u, "wq_grouped%d_%d" % (a, u), engines[u]) for u in range(2)]

        def quantize_wq(grouped, a):
            return [quantize(grouped[u], "wq%d_%d" % (a, u)) for u in range(2)]

        def quantize_x(grouped, a, tag=None):
            codes, plane = quantize(grouped, "x%d" % a, tag)
            return [(codes[:, mb * P : (mb + 1) * P], plane[:, mb * P : (mb + 1) * P]) for mb in range(M // P)]

        gather_words(0, HALF, 0)
        gather_words(HALF, BANK, BANK)
        part_words(0, HALF, 0)
        gather_words(BANK, J, 0)
        part_words(HALF, HALF + P, BANK)
        part_words(HALF + P, BANK, BANK + P)
        part_words(BANK, BANK + HALF, 0)
        part_words(BANK + HALF, J, HALF)
        deal_wk_words()
        x_first = interleave(x_raw[0][:], "x_grouped0", on_scalar)
        wv_first = [group_wv(0, 0, HALF), group_wv(0, HALF, N)]
        ka_grouped = [keys(tab_codes[h], h) for h in range(HALVES)]
        x_mx = [quantize_x(x_first, 0)]
        wv_mx = [quantize_wv(wv_first[0], "wv0_0") + quantize_wv(wv_first[1], "wv0_2")]
        wv_last = [group_wv(1, 0, P), group_wv(1, P, HALF)]
        wv_mx.append(quantize_wv(wv_last[0], "wv1_0"))
        wv_last.append(group_wv(1, HALF, N))
        wv_mx[1].extend(quantize_wv(wv_last[1], "wv1_1") + quantize_wv(wv_last[2], "wv1_2"))
        ka_mx = [quantize_keys(ka_grouped[0][0:2], "ka0", "wv_grouped1_1")]
        for nb in range(2):
            values(nb)
        wq_mx = [quantize_wq(group_wq(0, on_vector), 0)]
        wq_last = group_wq(1, on_scalar)
        for nb in range(2, N // P):
            values(nb)
        x_last = interleave(x_raw[1][:, :, 0:P], "x_grouped1_0", on_vector)
        wq_mx.append(quantize_wq(wq_last, 1))
        x_mx.append([quantize(x_last, "x1_0")])
        x_rest = interleave(x_raw[1][:, :, P:M], "x_grouped1_1", on_vector)
        ka_mx.append(quantize_keys(ka_grouped[0][2:4], "ka1", "x_grouped1_0"))
        x_mx[1].append(quantize(x_rest, "x1_1"))
        qa_grouped = [queries(mb) for mb in range(M // P)]
        qa_mx = [quantize(qa_grouped[mb], "qa%d" % mb) for mb in range(M // P)]
        ka_mx.append(quantize_keys(ka_grouped[1][0:2], "ka2", "qa_grouped0"))
        ka_mx.append(quantize_keys(ka_grouped[1][2:4], "ka3", "x_grouped1_1"))
        for mb in range(M // P):
            scores(qa_mx[mb], mb)
